import numpy as np
import ml_dtypes


def mxq(x, axis, fmt="e4m3"):
    dtype, down = {"e4m3": (ml_dtypes.float8_e4m3fn, 7), "e5m2": (ml_dtypes.float8_e5m2, 14)}[fmt]
    v = np.moveaxis(np.asarray(x, np.float32).astype(ml_dtypes.bfloat16).astype(np.float64), axis, -1)
    blocks = v.reshape(v.shape[:-1] + (-1, 32))
    amax = np.abs(blocks).max(-1, keepdims=True)
    byte = np.maximum(np.where(amax > 0, np.frexp(amax)[1] - 1 + 127, 0) - down, 1)
    scale = np.exp2(byte - 127.0)
    codes = (blocks / scale).astype(np.float32).astype(dtype).astype(np.float64)
    return np.moveaxis((codes * scale).reshape(v.shape), -1, axis)


WIDE = False


def mx_kscale(k):
    if not WIDE:
        return np.ones(k)
    levels = np.array([10, -10, 5, -5, 0])
    if k % 512:
        return np.exp2(np.random.permutation(np.resize(levels, k // 32))).repeat(32)
    a = np.empty((k // 512, 16))
    for p in range(k // 512):
        a[p, :8] = np.random.permutation(np.resize(levels, 8))
        for g in range(8):
            far = levels[np.abs(levels - a[p, g]) >= 10]
            a[p, g + 8] = far[np.random.randint(len(far))]
    return np.exp2(a.ravel()).repeat(32)


def f64(x):
    return np.asarray(x).astype(np.float64)


E2M1 = np.array([0.0, 0.5, 1.0, 1.5, 2.0, 3.0, 4.0, 6.0, -0.0, -0.5, -1.0, -1.5, -2.0, -3.0, -4.0, -6.0])


def pack_weight(w, fmt):
    k, n = w.shape
    w = f64(np.asarray(w, np.float32).astype(ml_dtypes.bfloat16)).reshape(k // 32, 32, n)
    amax = np.abs(w).max(1)
    if fmt == "e4m3":
        byte = np.frexp(amax)[1] - 1 + 127 - 7
    else:
        mant, ex = np.frexp(amax / 6.0)
        byte = np.where(mant > 0.5, ex, ex - 1) + 127
    byte = np.clip(np.where(amax > 0, byte, 1), 1, 254)
    scaled = (w * np.exp2(127.0 - byte)[:, None, :]).reshape(k, n).astype(np.float32)
    by_word = np.ascontiguousarray(scaled.reshape(k // 512, 128, 4, n).transpose(0, 1, 3, 2))
    if fmt == "e4m3":
        words = by_word.astype(ml_dtypes.float8_e4m3fn).view(np.uint8)
    else:
        c = by_word.astype(ml_dtypes.float4_e2m1fn).view(np.uint8) & 0xF
        words = (c[..., 0::2] | (c[..., 1::2] << 4)).reshape(k // 512, 128, 2 * n)
    return np.ascontiguousarray(words), np.ascontiguousarray(byte.astype(np.uint8).reshape(k // 512, 16, n))


def unpack_weight(words, scales, fmt):
    g, _, n = scales.shape
    words = np.ascontiguousarray(words).reshape(g, 128, n, -1)
    if fmt == "e4m3":
        vals = words.view(ml_dtypes.float8_e4m3fn).astype(np.float64)
    else:
        nib = np.empty((g, 128, n, 4), np.uint8)
        nib[..., 0::2] = words & 0xF
        nib[..., 1::2] = words >> 4
        vals = E2M1[nib]
    vals = vals * np.repeat(np.exp2(scales.astype(np.float64) - 127.0), 8, axis=1)[..., None]
    return vals.transpose(0, 1, 3, 2).reshape(g * 512, n)


K, R, M, T = 1024, 512, 1024, 1024


def setup_inputs():
    n = np.random.standard_normal
    s = mx_kscale(K)[:, None]
    u = mx_kscale(R)[:, None]
    p_w4 = pack_weight(n((K, M)) / np.sqrt(K) / s, "e2m1")
    return {
        "x": (n((K, T)) * s).astype(np.float32),
        "w4_words": p_w4[0],
        "w4_scales": p_w4[1],
        "down": (n((K, R)) / np.sqrt(K) / s * u.T).astype(np.float32),
        "up": (0.5 * n((R, M)) / np.sqrt(R) / u).astype(np.float32),
    }


def reference(x, w4_words, w4_scales, down, up):
    x_ = mxq(f64(x), 0, "e4m3")
    w4_ = unpack_weight(w4_words, w4_scales, "e2m1")
    down_ = mxq(f64(down), 0, "e4m3")
    up_ = mxq(f64(up), 0, "e4m3")
    h_ = mxq(down_.T @ x_, 0, "e4m3")
    y = x_.T @ w4_ + h_.T @ up_
    return y

@@ -1,0 +1,321 @@
+from contextlib import ExitStack
+
+import concourse.mybir as mybir
+
+K, R, N, T = 1024, 512, 1024, 1024
+FLOPS = 2 * (K * R * T + K * N * T + R * N * T)
+
+F32 = mybir.dt.float32
+BF16 = mybir.dt.bfloat16
+I32 = mybir.dt.int32
+U32 = mybir.dt.uint32
+U8 = mybir.dt.uint8
+E4M3 = mybir.dt.float8_e4m3fn_x4
+E2M1 = mybir.dt.float4_e2m1fn_x4
+
+P = 128
+PACK = 4
+ROWS = P * PACK
+K_PASSES = K // ROWS
+WIDTH = 256
+TILES_IN_CHUNK = WIDTH // P
+HALF = 512
+BANKS = 8
+
+
+def tile_mix_lowrank_tm_none_kernel(tc, x, w4_words, w4_scales, down, up, out):
+    nc = tc.nc
+    SCALAR, VECTOR = "scalar", "vector"
+
+    with ExitStack() as ctx:
+        keep = ctx.enter_context(tc.tile_pool(name="keep", bufs=1))
+        psum = ctx.enter_context(tc.psum_pool(name="psum", bufs=1))
+        ctx.enter_context(tc.manual_schedule())
+
+        def sbuf(name, shape, dtype):
+            return keep.tile(shape, dtype, name=name, tag=name, align_bytes=64)
+
+        free_banks = list(range(BANKS))
+        bank_of = {}
+
+        def take_bank(key, name, shape):
+            bank_of[key] = free_banks[0]
+            free_banks.remove(bank_of[key])
+            return psum.tile(shape, F32, name=name, tag=f"bank{bank_of[key]}")
+
+        def give_back(key):
+            free_banks.append(bank_of[key])
+
+        def copy(engine, dst, src):
+            if engine == SCALAR:
+                nc.scalar.copy(out=dst, in_=src)
+            else:
+                nc.vector.tensor_copy(out=dst, in_=src)
+
+        def quantise(name, width, grouped):
+            codes = sbuf(f"{name}_codes", [P, width], U32)
+            scales = sbuf(f"{name}_scales", [P, width], U8)
+            nc.vector.quantize_mx(out=codes[:].bitcast(E4M3), scales=scales[:], in_=grouped)
+            return codes, scales
+
+        def interleave(engine, grouped, raw):
+            copy(
+                engine,
+                grouped.rearrange("p (c i) j -> p c j i", i=4),
+                raw.rearrange("p j (c i) -> p c j i", i=4),
+            )
+
+        x_raw, x_grouped, x_mx = {}, {}, {}
+
+        def load_x(c, g):
+            x_raw[c, g] = sbuf(f"x{c}{g}_raw", [P, PACK, WIDTH], F32)
+            rows = x[g * ROWS : (g + 1) * ROWS, c * WIDTH : (c + 1) * WIDTH]
+            nc.sync.dma_start(out=x_raw[c, g][:], in_=rows.rearrange("(p j) t -> p j t", j=PACK))
+
+        def interleave_x(c, g, engine):
+            x_grouped[c, g] = sbuf(f"x{c}{g}_grouped", [P, WIDTH, PACK], BF16)
+            interleave(engine, x_grouped[c, g][:], x_raw[c, g][:])
+
+        def quantise_x(c, g):
+            x_mx[c, g] = quantise(f"x{c}{g}", WIDTH, x_grouped[c, g][:].rearrange("p t j -> p (t j)"))
+
+        def x_tile(t, g):
+            codes, scales = x_mx[t // TILES_IN_CHUNK, g]
+            first = (t % TILES_IN_CHUNK) * P
+            return codes[:, first : first + P].bitcast(E4M3), scales[:, first : first + P]
+
+        down_raw, down_grouped, down_mx = {}, {}, {}
+
+        def load_down(g):
+            down_raw[g] = sbuf(f"down{g}_raw", [P, PACK, R], F32)
+            rows = down[g * ROWS : (g + 1) * ROWS, :]
+            nc.sync.dma_start(out=down_raw[g][:], in_=rows.rearrange("(p j) r -> p j r", j=PACK))
+
+        def interleave_down(g):
+            down_grouped[g] = sbuf(f"down{g}_grouped", [P, PACK, P, PACK], BF16)
+            grouped = down_grouped[g][:].rearrange("p i m j -> p m i j")
+            raw = down_raw[g][:].rearrange("p j (m i) -> p m i j", i=PACK)
+            middle = P // 2
+            copy(VECTOR, grouped[:, :middle], raw[:, :middle])
+            copy(SCALAR, grouped[:, middle:], raw[:, middle:])
+
+        def quantise_down(g):
+            down_mx[g] = quantise(f"down{g}", R, down_grouped[g][:].rearrange("p i m j -> p (i m j)"))
+
+        up_raw, up_grouped = {}, {}
+        up_codes = [sbuf(f"up{n}_codes", [P, HALF], U32) for n in range(2)]
+        up_scales = [sbuf(f"up{n}_scales", [P, HALF], U8) for n in range(2)]
+
+        def load_up(q):
+            up_raw[q] = sbuf(f"up{q}_raw", [P, PACK, WIDTH], F32)
+            rows = up[:, q * WIDTH : (q + 1) * WIDTH]
+            nc.sync.dma_start(out=up_raw[q][:], in_=rows.rearrange("(p j) n -> p j n", j=PACK))
+
+        def interleave_up(q, engine):
+            up_grouped[q] = sbuf(f"up{q}_grouped", [P, WIDTH, PACK], BF16)
+            interleave(engine, up_grouped[q][:], up_raw[q][:])
+
+        def quantise_up(q):
+            n, first = q // 2, (q % 2) * WIDTH
+            nc.vector.quantize_mx(
+                out=up_codes[n][:, first : first + WIDTH].bitcast(E4M3),
+                scales=up_scales[n][:, first : first + WIDTH],
+                in_=up_grouped[q][:].rearrange("p n j -> p (n j)"),
+            )
+
+        w4_codes = sbuf("w4_codes", [P, K_PASSES, 2 * N], U8)
+        w4_planes = sbuf("w4_planes", [P, K_PASSES, N], U8)
+
+        def load_w4():
+            for quadrant in range(4):
+                nc.sync.dma_start(
+                    out=w4_planes[32 * quadrant : 32 * quadrant + 4].bitcast(I32),
+                    in_=w4_scales[:, 4 * quadrant : 4 * quadrant + 4, :].rearrange("g s n -> s g n").bitcast(I32),
+                )
+            nc.sync.dma_start(out=w4_codes[:].bitcast(I32), in_=w4_words.rearrange("g p n -> p g n").bitcast(I32))
+
+        h_sums, h_grouped, h_mx = {}, {}, {}
+
+        def make_h(t):
+            h_sums[t] = take_bank(("h", t), f"h{t}_sums", [P, PACK, P])
+            for i in range(PACK):
+                for g in range(K_PASSES):
+                    down_codes, down_scales = down_mx[g]
+                    codes, scales = x_tile(t, g)
+                    nc.tensor.matmul_mx(
+                        out=h_sums[t][:, i, :],
+                        lhsT=down_codes[:, i * P : (i + 1) * P].bitcast(E4M3),
+                        lhsT_scale=down_scales[:, i * P : (i + 1) * P],
+                        rhs=codes,
+                        rhs_scale=scales,
+                        start=(g == 0),
+                        stop=(g == K_PASSES - 1),
+                    )
+
+        def empty_h(t, engine):
+            h_grouped[t] = sbuf(f"h{t}_grouped", [P, P, PACK], BF16)
+            copy(engine, h_grouped[t][:], h_sums[t][:].rearrange("p i t -> p t i"))
+            give_back(("h", t))
+
+        def quantise_h(t):
+            h_mx[t] = quantise(f"h{t}", P, h_grouped[t][:].rearrange("p t i -> p (t i)"))
+
+        sums = {}
+
+        def base(t, n):
+            sums[t, n] = take_bank((t, n), f"sums{t}{n}", [P, HALF])
+            for g in range(K_PASSES):
+                codes, scales = x_tile(t, g)
+                nc.tensor.matmul_mx(
+                    out=sums[t, n][:],
+                    lhsT=codes,
+                    lhsT_scale=scales,
+                    rhs=w4_codes[:, g, 2 * HALF * n : 2 * HALF * (n + 1)].bitcast(E2M1),
+                    rhs_scale=w4_planes[:, g, HALF * n : HALF * (n + 1)],
+                    start=(g == 0),
+                    stop=False,
+                )
+
+        def branch(t, n):
+            codes, scales = h_mx[t]
+            nc.tensor.matmul_mx(
+                out=sums[t, n][:],
+                lhsT=codes[:].bitcast(E4M3),
+                lhsT_scale=scales[:],
+                rhs=up_codes[n][:].bitcast(E4M3),
+                rhs_scale=up_scales[n][:],
+                start=False,
+                stop=True,
+            )
+
+        def finish(t, n, engine, parts=1):
+            width = HALF // parts
+            for i in range(parts):
+                part = sbuf(f"result{t}{n}{i}", [P, width], F32)
+                copy(engine, part[:], sums[t, n][:, i * width : (i + 1) * width])
+                first = n * HALF + i * width
+                nc.sync.dma_start(out=out[t * P : (t + 1) * P, first : first + width], in_=part[:])
+            give_back((t, n))
+
+        nc.vector.memset(w4_planes[:].rearrange("p g n -> p (g n)").bitcast(I32), 0)
+
+        load_down(0)
+        load_x(0, 0)
+        load_x(0, 1)
+        load_down(1)
+        load_w4()
+        load_x(1, 0)
+        load_x(1, 1)
+        load_up(0)
+        load_up(1)
+        load_x(2, 0)
+        load_x(2, 1)
+        load_x(3, 0)
+        load_up(2)
+        load_up(3)
+        load_x(3, 1)
+
+        interleave_down(0)
+        quantise_down(0)
+        interleave_x(0, 0, SCALAR)
+        interleave_x(0, 1, VECTOR)
+        quantise_x(0, 0)
+        quantise_x(0, 1)
+        interleave_down(1)
+        base(0, 0)
+        quantise_down(1)
+        base(0, 1)
+
+        interleave_x(1, 0, SCALAR)
+        make_h(0)
+        interleave_x(1, 1, VECTOR)
+        make_h(1)
+        empty_h(0, SCALAR)
+        base(1, 0)
+        quantise_x(1, 0)
+        empty_h(1, SCALAR)
+        base(1, 1)
+        quantise_x(1, 1)
+        quantise_h(0)
+        interleave_up(0, SCALAR)
+        quantise_h(1)
+        base(2, 0)
+        interleave_up(1, VECTOR)
+        base(3, 1)
+        make_h(3)
+        quantise_up(0)
+
+        interleave_x(2, 0, SCALAR)
+        quantise_up(1)
+        make_h(2)
+        empty_h(3, VECTOR)
+        branch(0, 0)
+        branch(1, 0)
+        interleave_x(2, 1, VECTOR)
+        empty_h(2, SCALAR)
+        base(3, 0)
+        quantise_h(3)
+        finish(0, 0, SCALAR)
+        quantise_h(2)
+        branch(3, 0)
+        quantise_x(2, 0)
+        branch(2, 0)
+        finish(1, 0, SCALAR)
+        quantise_x(2, 1)
+        base(2, 1)
+
+        interleave_up(2, VECTOR)
+        finish(2, 0, SCALAR)
+        make_h(4)
+        finish(3, 0, SCALAR)
+        base(5, 0)
+        quantise_up(2)
+        base(4, 1)
+        interleave_up(3, VECTOR)
+        empty_h(4, SCALAR)
+        make_h(5)
+        interleave_x(3, 0, SCALAR)
+        quantise_up(3)
+        base(4, 0)
+        quantise_h(4)
+        interleave_x(3, 1, VECTOR)
+        branch(3, 1)
+        branch(2, 1)
+        empty_h(5, SCALAR)
+        quantise_x(3, 0)
+        branch(0, 1)
+        branch(1, 1)
+        quantise_x(3, 1)
+        finish(3, 1, SCALAR)
+        branch(4, 1)
+        finish(1, 1, VECTOR)
+        branch(4, 0)
+        finish(0, 1, SCALAR)
+
+        make_h(6)
+        quantise_h(5)
+        base(6, 1)
+        finish(4, 1, SCALAR)
+        empty_h(6, VECTOR)
+        make_h(7)
+        finish(2, 1, SCALAR)
+        quantise_h(6)
+        base(7, 0)
+        empty_h(7, SCALAR)
+        branch(6, 1)
+        base(7, 1)
+        finish(4, 0, SCALAR)
+        finish(6, 1, VECTOR)
+        branch(5, 0)
+        quantise_h(7)
+        base(5, 1)
+        finish(5, 0, SCALAR)
+        branch(7, 1)
+        branch(7, 0)
+        finish(7, 1, VECTOR)
+        branch(5, 1)
+        finish(7, 0, SCALAR)
+        base(6, 0)
+        finish(5, 1, VECTOR)
+        branch(6, 0)
+        finish(6, 0, VECTOR, parts=2)

@@ -65,44 +65,76 @@ def tile_mix_lowrank_tm_none_kernel(tc, x, w4_words, w4_scales, down, up, out):
                 raw.rearrange("p j (c i) -> p c j i", i=4),
             )
 
-        x_raw, x_grouped, x_mx = {}, {}, {}
+        x_raw, x_mx = {}, {}
 
         def load_x(c, g):
             x_raw[c, g] = sbuf(f"x{c}{g}_raw", [P, PACK, WIDTH], F32)
             rows = x[g * ROWS : (g + 1) * ROWS, c * WIDTH : (c + 1) * WIDTH]
             nc.sync.dma_start(out=x_raw[c, g][:], in_=rows.rearrange("(p j) t -> p j t", j=PACK))
 
-        def interleave_x(c, g, engine):
-            x_grouped[c, g] = sbuf(f"x{c}{g}_grouped", [P, WIDTH, PACK], BF16)
-            interleave(engine, x_grouped[c, g][:], x_raw[c, g][:])
+        def prepare(name, raw, codes, scales, scalar_columns, between):
+            grouped = sbuf(f"{name}_grouped", [P, WIDTH, PACK], BF16)
 
-        def quantise_x(c, g):
-            x_mx[c, g] = quantise(f"x{c}{g}", WIDTH, x_grouped[c, g][:].rearrange("p t j -> p (t j)"))
+            def quantise_columns(first, count):
+                nc.vector.quantize_mx(
+                    out=codes[:, first : first + count].bitcast(E4M3),
+                    scales=scales[:, first : first + count],
+                    in_=grouped[:, first : first + count].rearrange("p c j -> p (c j)"),
+                )
+
+            if scalar_columns:
+                split = WIDTH - scalar_columns
+                interleave(VECTOR, grouped[:, :split], raw[:, :, :split])
+                interleave(SCALAR, grouped[:, split:], raw[:, :, split:])
+                if between is not None:
+                    quantise_h(between)
+                quantise_columns(0, WIDTH)
+            else:
+                interleave(VECTOR, grouped[:, :P], raw[:, :, :P])
+                interleave(VECTOR, grouped[:, P:], raw[:, :, P:])
+                quantise_columns(0, P)
+                if between is not None:
+                    quantise_h(between)
+                quantise_columns(P, P)
+
+        def prepare_x(c, g, scalar_columns=0, between=None):
+            codes = sbuf(f"x{c}{g}_codes", [P, WIDTH], U32)
+            scales = sbuf(f"x{c}{g}_scales", [P, WIDTH], U8)
+            x_mx[c, g] = codes, scales
+            prepare(f"x{c}{g}", x_raw[c, g], codes[:], scales[:], scalar_columns, between)
 
         def x_tile(t, g):
             codes, scales = x_mx[t // TILES_IN_CHUNK, g]
             first = (t % TILES_IN_CHUNK) * P
             return codes[:, first : first + P].bitcast(E4M3), scales[:, first : first + P]
 
-        down_raw, down_grouped, down_mx = {}, {}, {}
+        down_raw = {}
+        down_grouped = [sbuf(f"down{g}_grouped", [P, PACK, P, PACK], BF16) for g in range(K_PASSES)]
+        down_codes = [sbuf(f"down{g}_codes", [P, R], U32) for g in range(K_PASSES)]
+        down_scales = [sbuf(f"down{g}_scales", [P, R], U8) for g in range(K_PASSES)]
 
-        def load_down(g):
-            down_raw[g] = sbuf(f"down{g}_raw", [P, PACK, R], F32)
-            rows = down[g * ROWS : (g + 1) * ROWS, :]
-            nc.sync.dma_start(out=down_raw[g][:], in_=rows.rearrange("(p j) r -> p j r", j=PACK))
+        def load_down(g, first, count):
+            down_raw[g, first] = sbuf(f"down{g}{first}_raw", [P, PACK, PACK * count], F32)
+            rows = down[g * ROWS : (g + 1) * ROWS, PACK * first : PACK * (first + count)]
+            nc.sync.dma_start(out=down_raw[g, first][:], in_=rows.rearrange("(p j) r -> p j r", j=PACK))
 
-        def interleave_down(g):
-            down_grouped[g] = sbuf(f"down{g}_grouped", [P, PACK, P, PACK], BF16)
-            grouped = down_grouped[g][:].rearrange("p i m j -> p m i j")
-            raw = down_raw[g][:].rearrange("p j (m i) -> p m i j", i=PACK)
-            middle = P // 2
-            copy(VECTOR, grouped[:, :middle], raw[:, :middle])
-            copy(SCALAR, grouped[:, middle:], raw[:, middle:])
+        def interleave_down(g, first, count, scalar_count):
+            grouped = down_grouped[g][:].rearrange("p i m j -> p m i j")[:, first : first + count]
+            raw = down_raw[g, first][:].rearrange("p j (m i) -> p m i j", i=PACK)
+            split = count - scalar_count
+            copy(VECTOR, grouped[:, :split], raw[:, :split])
+            if scalar_count:
+                copy(SCALAR, grouped[:, split:], raw[:, split:])
 
-        def quantise_down(g):
-            down_mx[g] = quantise(f"down{g}", R, down_grouped[g][:].rearrange("p i m j -> p (i m j)"))
+        def quantise_down(g, first, count):
+            grouped = down_grouped[g][:].rearrange("p i m j -> p (i m j)")
+            nc.vector.quantize_mx(
+                out=down_codes[g][:, first : first + count].bitcast(E4M3),
+                scales=down_scales[g][:, first : first + count],
+                in_=grouped[:, PACK * first : PACK * (first + count)],
+            )
 
-        up_raw, up_grouped = {}, {}
+        up_raw = {}
         up_codes = [sbuf(f"up{n}_codes", [P, HALF], U32) for n in range(2)]
         up_scales = [sbuf(f"up{n}_scales", [P, HALF], U8) for n in range(2)]
 
@@ -111,46 +143,39 @@ def tile_mix_lowrank_tm_none_kernel(tc, x, w4_words, w4_scales, down, up, out):
             rows = up[:, q * WIDTH : (q + 1) * WIDTH]
             nc.sync.dma_start(out=up_raw[q][:], in_=rows.rearrange("(p j) n -> p j n", j=PACK))
 
-        def interleave_up(q, engine):
-            up_grouped[q] = sbuf(f"up{q}_grouped", [P, WIDTH, PACK], BF16)
-            interleave(engine, up_grouped[q][:], up_raw[q][:])
-
-        def quantise_up(q):
-            n, first = q // 2, (q % 2) * WIDTH
-            nc.vector.quantize_mx(
-                out=up_codes[n][:, first : first + WIDTH].bitcast(E4M3),
-                scales=up_scales[n][:, first : first + WIDTH],
-                in_=up_grouped[q][:].rearrange("p n j -> p (n j)"),
-            )
+        def prepare_up(q, scalar_columns=0, between=None):
+            n, columns = q // 2, slice((q % 2) * WIDTH, (q % 2 + 1) * WIDTH)
+            prepare(f"up{q}", up_raw[q], up_codes[n][:, columns], up_scales[n][:, columns], scalar_columns, between)
 
         w4_codes = sbuf("w4_codes", [P, K_PASSES, 2 * N], U8)
         w4_planes = sbuf("w4_planes", [P, K_PASSES, N], U8)
 
-        def load_w4():
+        def load_w4_scales():
             for quadrant in range(4):
                 nc.sync.dma_start(
                     out=w4_planes[32 * quadrant : 32 * quadrant + 4].bitcast(I32),
                     in_=w4_scales[:, 4 * quadrant : 4 * quadrant + 4, :].rearrange("g s n -> s g n").bitcast(I32),
                 )
+
+        def load_w4_codes():
             nc.sync.dma_start(out=w4_codes[:].bitcast(I32), in_=w4_words.rearrange("g p n -> p g n").bitcast(I32))
 
         h_sums, h_grouped, h_mx = {}, {}, {}
 
-        def make_h(t):
-            h_sums[t] = take_bank(("h", t), f"h{t}_sums", [P, PACK, P])
+        def make_h(t, g):
+            if g == 0:
+                h_sums[t] = take_bank(("h", t), f"h{t}_sums", [P, PACK, P])
+            codes, scales = x_tile(t, g)
             for i in range(PACK):
-                for g in range(K_PASSES):
-                    down_codes, down_scales = down_mx[g]
-                    codes, scales = x_tile(t, g)
-                    nc.tensor.matmul_mx(
-                        out=h_sums[t][:, i, :],
-                        lhsT=down_codes[:, i * P : (i + 1) * P].bitcast(E4M3),
-                        lhsT_scale=down_scales[:, i * P : (i + 1) * P],
-                        rhs=codes,
-                        rhs_scale=scales,
-                        start=(g == 0),
-                        stop=(g == K_PASSES - 1),
-                    )
+                nc.tensor.matmul_mx(
+                    out=h_sums[t][:, i, :],
+                    lhsT=down_codes[g][:, i * P : (i + 1) * P].bitcast(E4M3),
+                    lhsT_scale=down_scales[g][:, i * P : (i + 1) * P],
+                    rhs=codes,
+                    rhs_scale=scales,
+                    start=(g == 0 and i == 0),
+                    stop=(g == K_PASSES - 1 and i == PACK - 1),
+                )
 
         def empty_h(t, engine):
             h_grouped[t] = sbuf(f"h{t}_grouped", [P, P, PACK], BF16)
@@ -162,19 +187,19 @@ def tile_mix_lowrank_tm_none_kernel(tc, x, w4_words, w4_scales, down, up, out):
 
         sums = {}
 
-        def base(t, n):
-            sums[t, n] = take_bank((t, n), f"sums{t}{n}", [P, HALF])
-            for g in range(K_PASSES):
-                codes, scales = x_tile(t, g)
-                nc.tensor.matmul_mx(
-                    out=sums[t, n][:],
-                    lhsT=codes,
-                    lhsT_scale=scales,
-                    rhs=w4_codes[:, g, 2 * HALF * n : 2 * HALF * (n + 1)].bitcast(E2M1),
-                    rhs_scale=w4_planes[:, g, HALF * n : HALF * (n + 1)],
-                    start=(g == 0),
-                    stop=False,
-                )
+        def base(t, n, g):
+            if g == 0:
+                sums[t, n] = take_bank((t, n), f"sums{t}{n}", [P, HALF])
+            codes, scales = x_tile(t, g)
+            nc.tensor.matmul_mx(
+                out=sums[t, n][:],
+                lhsT=codes,
+                lhsT_scale=scales,
+                rhs=w4_codes[:, g, 2 * HALF * n : 2 * HALF * (n + 1)].bitcast(E2M1),
+                rhs_scale=w4_planes[:, g, HALF * n : HALF * (n + 1)],
+                start=(g == 0),
+                stop=False,
+            )
 
         def branch(t, n):
             codes, scales = h_mx[t]
@@ -188,134 +213,183 @@ def tile_mix_lowrank_tm_none_kernel(tc, x, w4_words, w4_scales, down, up, out):
                 stop=True,
             )
 
-        def finish(t, n, engine, parts=1):
-            width = HALF // parts
-            for i in range(parts):
-                part = sbuf(f"result{t}{n}{i}", [P, width], F32)
-                copy(engine, part[:], sums[t, n][:, i * width : (i + 1) * width])
-                first = n * HALF + i * width
-                nc.sync.dma_start(out=out[t * P : (t + 1) * P, first : first + width], in_=part[:])
+        results = {}
+
+        def empty(t, n, engine):
+            c = t // TILES_IN_CHUNK
+            if (c, n) not in results:
+                results[c, n] = sbuf(f"result{c}{n}", [P, TILES_IN_CHUNK, HALF], F32)
+            copy(engine, results[c, n][:, t % TILES_IN_CHUNK, :], sums[t, n][:])
             give_back((t, n))
+
+        def store_chunk(c, n):
+            rows = out[c * WIDTH : (c + 1) * WIDTH, n * HALF : (n + 1) * HALF]
+            nc.sync.dma_start(out=rows.rearrange("(t p) n -> p t n", p=P), in_=results[c, n][:])
+
+        def store_tile(t, n):
+            c = t // TILES_IN_CHUNK
+            rows = out[t * P : (t + 1) * P, n * HALF : (n + 1) * HALF]
+            nc.sync.dma_start(out=rows, in_=results[c, n][:, t % TILES_IN_CHUNK, :])
+
+        def last_half(t, n):
+            h_codes, h_scales = h_mx[t]
+            for part, engine in enumerate((SCALAR, VECTOR)):
+                bank = take_bank((t, n, part), f"last{part}", [P, WIDTH])
+                for s in range(WIDTH // P):
+                    first = n * HALF + part * WIDTH + s * P
+                    for g in range(K_PASSES):
+                        codes, scales = x_tile(t, g)
+                        nc.tensor.matmul_mx(
+                            out=bank[:, s * P : (s + 1) * P],
+                            lhsT=codes,
+                            lhsT_scale=scales,
+                            rhs=w4_codes[:, g, 2 * first : 2 * (first + P)].bitcast(E2M1),
+                            rhs_scale=w4_planes[:, g, first : first + P],
+                            start=(g == 0 and s == 0),
+                            stop=False,
+                        )
+                nc.tensor.matmul_mx(
+                    out=bank[:],
+                    lhsT=h_codes[:].bitcast(E4M3),
+                    lhsT_scale=h_scales[:],
+                    rhs=up_codes[n][:, part * WIDTH : (part + 1) * WIDTH].bitcast(E4M3),
+                    rhs_scale=up_scales[n][:, part * WIDTH : (part + 1) * WIDTH],
+                    start=False,
+                    stop=True,
+                )
+                result = sbuf(f"last{part}_result", [P, WIDTH], F32)
+                copy(engine, result[:], bank[:])
+                first = n * HALF + part * WIDTH
+                nc.sync.dma_start(out=out[t * P : (t + 1) * P, first : first + WIDTH], in_=result[:])
 
         nc.vector.memset(w4_planes[:].rearrange("p g n -> p (g n)").bitcast(I32), 0)
 
-        load_down(0)
         load_x(0, 0)
         load_x(0, 1)
-        load_down(1)
-        load_w4()
-        load_x(1, 0)
-        load_x(1, 1)
+        load_down(0, 0, P)
+        load_w4_scales()
+        load_w4_codes()
+        load_down(1, 0, P // 2)
+        load_down(1, P // 2, P // 2)
+        for g in range(K_PASSES):
+            load_x(1, g)
         load_up(0)
         load_up(1)
-        load_x(2, 0)
-        load_x(2, 1)
-        load_x(3, 0)
+        for g in range(K_PASSES):
+            load_x(2, g)
         load_up(2)
         load_up(3)
-        load_x(3, 1)
+        for g in range(K_PASSES):
+            load_x(3, g)
 
-        interleave_down(0)
-        quantise_down(0)
-        interleave_x(0, 0, SCALAR)
-        interleave_x(0, 1, VECTOR)
-        quantise_x(0, 0)
-        quantise_x(0, 1)
-        interleave_down(1)
-        base(0, 0)
-        quantise_down(1)
-        base(0, 1)
+        for g in range(K_PASSES):
+            prepare_x(0, g, 96)
+        interleave_down(0, 0, P, 44)
+        quantise_down(0, 0, R)
+        for t in (0, 1):
+            for n in range(2):
+                for g in range(K_PASSES):
+                    base(t, n, g)
+        make_h(0, 0)
+        make_h(1, 0)
+        for first in (0, P // 2):
+            interleave_down(1, first, P // 2, 24)
+            for i in range(PACK):
+                quantise_down(1, i * P + first, P // 2)
+        make_h(0, 1)
+        make_h(1, 1)
 
-        interleave_x(1, 0, SCALAR)
-        make_h(0)
-        interleave_x(1, 1, VECTOR)
-        make_h(1)
+        prepare_x(1, 0, 96)
         empty_h(0, SCALAR)
-        base(1, 0)
-        quantise_x(1, 0)
         empty_h(1, SCALAR)
-        base(1, 1)
-        quantise_x(1, 1)
-        quantise_h(0)
-        interleave_up(0, SCALAR)
-        quantise_h(1)
-        base(2, 0)
-        interleave_up(1, VECTOR)
-        base(3, 1)
-        make_h(3)
-        quantise_up(0)
-
-        interleave_x(2, 0, SCALAR)
-        quantise_up(1)
-        make_h(2)
-        empty_h(3, VECTOR)
-        branch(0, 0)
-        branch(1, 0)
-        interleave_x(2, 1, VECTOR)
+        base(2, 0, 0)
+        base(3, 0, 0)
+        make_h(2, 0)
+        make_h(3, 0)
+        prepare_x(1, 1, between=0)
+        make_h(2, 1)
+        make_h(3, 1)
+        base(2, 0, 1)
+        base(3, 0, 1)
+        prepare_up(0, 96, between=1)
         empty_h(2, SCALAR)
-        base(3, 0)
-        quantise_h(3)
-        finish(0, 0, SCALAR)
-        quantise_h(2)
-        branch(3, 0)
-        quantise_x(2, 0)
-        branch(2, 0)
-        finish(1, 0, SCALAR)
-        quantise_x(2, 1)
-        base(2, 1)
+        empty_h(3, SCALAR)
+        base(2, 1, 0)
+        base(2, 1, 1)
+        base(3, 1, 0)
+        prepare_up(1, between=2)
+        for t in range(3):
+            branch(t, 0)
 
-        interleave_up(2, VECTOR)
-        finish(2, 0, SCALAR)
-        make_h(4)
-        finish(3, 0, SCALAR)
-        base(5, 0)
-        quantise_up(2)
-        base(4, 1)
-        interleave_up(3, VECTOR)
+        prepare_x(2, 0, 96, between=3)
+        branch(3, 0)
+        base(3, 1, 1)
+        for t in range(4):
+            empty(t, 0, SCALAR)
+        make_h(4, 0)
+        make_h(5, 0)
+        prepare_x(2, 1)
+        make_h(4, 1)
+        make_h(5, 1)
+        for t in (4, 5):
+            for g in range(K_PASSES):
+                base(t, 0, g)
         empty_h(4, SCALAR)
-        make_h(5)
-        interleave_x(3, 0, SCALAR)
-        quantise_up(3)
-        base(4, 0)
-        quantise_h(4)
-        interleave_x(3, 1, VECTOR)
-        branch(3, 1)
-        branch(2, 1)
         empty_h(5, SCALAR)
-        quantise_x(3, 0)
+        prepare_up(2)
+        prepare_up(3, between=4)
+        base(4, 1, 0)
+        base(4, 1, 1)
+        branch(4, 0)
         branch(0, 1)
         branch(1, 1)
-        quantise_x(3, 1)
-        finish(3, 1, SCALAR)
-        branch(4, 1)
-        finish(1, 1, VECTOR)
-        branch(4, 0)
-        finish(0, 1, SCALAR)
-
-        make_h(6)
-        quantise_h(5)
-        base(6, 1)
-        finish(4, 1, SCALAR)
-        empty_h(6, VECTOR)
-        make_h(7)
-        finish(2, 1, SCALAR)
-        quantise_h(6)
-        base(7, 0)
-        empty_h(7, SCALAR)
-        branch(6, 1)
-        base(7, 1)
-        finish(4, 0, SCALAR)
-        finish(6, 1, VECTOR)
+        prepare_x(3, 0, 96, between=5)
+        branch(2, 1)
+        branch(3, 1)
         branch(5, 0)
-        quantise_h(7)
-        base(5, 1)
-        finish(5, 0, SCALAR)
-        branch(7, 1)
-        branch(7, 0)
-        finish(7, 1, VECTOR)
+        branch(4, 1)
+        empty(4, 0, SCALAR)
+        empty(0, 1, SCALAR)
+        empty(1, 1, SCALAR)
+
+        make_h(6, 0)
+        prepare_x(3, 1)
+        make_h(6, 1)
+        base(5, 1, 0)
+        base(5, 1, 1)
         branch(5, 1)
-        finish(7, 0, SCALAR)
-        base(6, 0)
-        finish(5, 1, VECTOR)
+        empty(2, 1, SCALAR)
+        empty(3, 1, VECTOR)
+        empty(5, 0, SCALAR)
+        make_h(7, 0)
+        make_h(7, 1)
+        empty_h(6, VECTOR)
+        base(6, 0, 0)
+        base(6, 0, 1)
+        quantise_h(6)
         branch(6, 0)
-        finish(6, 0, VECTOR, parts=2)
+        empty(4, 1, SCALAR)
+        base(6, 1, 0)
+        base(6, 1, 1)
+        empty(5, 1, SCALAR)
+        empty_h(7, VECTOR)
+        branch(6, 1)
+        quantise_h(7)
+        base(7, 0, 0)
+        base(7, 0, 1)
+        branch(7, 0)
+        empty(6, 0, SCALAR)
+        empty(6, 1, VECTOR)
+        empty(7, 0, VECTOR)
+
+        store_chunk(0, 0)
+        store_chunk(1, 0)
+        store_tile(4, 0)
+        store_chunk(0, 1)
+        store_chunk(1, 1)
+        store_tile(5, 0)
+        store_chunk(2, 1)
+        store_tile(6, 0)
+        store_tile(6, 1)
+        store_tile(7, 0)
+        last_half(7, 1)

@@ -67,10 +67,12 @@ def tile_mix_lowrank_tm_none_kernel(tc, x, w4_words, w4_scales, down, up, out):
 
         x_raw, x_mx = {}, {}
 
-        def load_x(c, g):
-            x_raw[c, g] = sbuf(f"x{c}{g}_raw", [P, PACK, WIDTH], F32)
-            rows = x[g * ROWS : (g + 1) * ROWS, c * WIDTH : (c + 1) * WIDTH]
-            nc.sync.dma_start(out=x_raw[c, g][:], in_=rows.rearrange("(p j) t -> p j t", j=PACK))
+        def load_x(first, count, g):
+            raw = sbuf(f"x{first}{g}_raw", [P, PACK, count * WIDTH], F32)
+            rows = x[g * ROWS : (g + 1) * ROWS, first * WIDTH : (first + count) * WIDTH]
+            nc.sync.dma_start(out=raw[:], in_=rows.rearrange("(p j) t -> p j t", j=PACK))
+            for c in range(count):
+                x_raw[first + c, g] = raw[:, :, c * WIDTH : (c + 1) * WIDTH]
 
         def prepare(name, raw, codes, scales, scalar_columns, between):
             grouped = sbuf(f"{name}_grouped", [P, WIDTH, PACK], BF16)
@@ -138,14 +140,29 @@ def tile_mix_lowrank_tm_none_kernel(tc, x, w4_words, w4_scales, down, up, out):
         up_codes = [sbuf(f"up{n}_codes", [P, HALF], U32) for n in range(2)]
         up_scales = [sbuf(f"up{n}_scales", [P, HALF], U8) for n in range(2)]
 
-        def load_up(q):
-            up_raw[q] = sbuf(f"up{q}_raw", [P, PACK, WIDTH], F32)
-            rows = up[:, q * WIDTH : (q + 1) * WIDTH]
-            nc.sync.dma_start(out=up_raw[q][:], in_=rows.rearrange("(p j) n -> p j n", j=PACK))
+        def load_up(first, count):
+            raw = sbuf(f"up{first}_raw", [P, PACK, count * WIDTH], F32)
+            rows = up[:, first * WIDTH : (first + count) * WIDTH]
+            nc.sync.dma_start(out=raw[:], in_=rows.rearrange("(p j) n -> p j n", j=PACK))
+            for q in range(count):
+                up_raw[first + q] = raw[:, :, q * WIDTH : (q + 1) * WIDTH]
 
         def prepare_up(q, scalar_columns=0, between=None):
             n, columns = q // 2, slice((q % 2) * WIDTH, (q % 2 + 1) * WIDTH)
             prepare(f"up{q}", up_raw[q], up_codes[n][:, columns], up_scales[n][:, columns], scalar_columns, between)
+
+        def interleave_up_shared():
+            grouped = sbuf("up_right_grouped", [P, HALF, PACK], BF16)
+            split = 64
+            interleave(VECTOR, grouped[:, :WIDTH], up_raw[2])
+            interleave(VECTOR, grouped[:, WIDTH : WIDTH + split], up_raw[3][:, :, :split])
+            interleave(SCALAR, grouped[:, WIDTH + split :], up_raw[3][:, :, split:])
+            for first in (0, WIDTH):
+                nc.vector.quantize_mx(
+                    out=up_codes[1][:, first : first + WIDTH].bitcast(E4M3),
+                    scales=up_scales[1][:, first : first + WIDTH],
+                    in_=grouped[:, first : first + WIDTH].rearrange("p c j -> p (c j)"),
+                )
 
         w4_codes = sbuf("w4_codes", [P, K_PASSES, 2 * N], U8)
         w4_planes = sbuf("w4_planes", [P, K_PASSES, N], U8)
@@ -216,24 +233,21 @@ def tile_mix_lowrank_tm_none_kernel(tc, x, w4_words, w4_scales, down, up, out):
         results = {}
 
         def empty(t, n, engine):
-            c = t // TILES_IN_CHUNK
-            if (c, n) not in results:
-                results[c, n] = sbuf(f"result{c}{n}", [P, TILES_IN_CHUNK, HALF], F32)
-            copy(engine, results[c, n][:, t % TILES_IN_CHUNK, :], sums[t, n][:])
+            if t not in results:
+                results[t] = sbuf(f"result{t}", [P, N], F32)
+            copy(engine, results[t][:, n * HALF : (n + 1) * HALF], sums[t, n][:])
             give_back((t, n))
 
-        def store_chunk(c, n):
-            rows = out[c * WIDTH : (c + 1) * WIDTH, n * HALF : (n + 1) * HALF]
-            nc.sync.dma_start(out=rows.rearrange("(t p) n -> p t n", p=P), in_=results[c, n][:])
+        def store_tile(t):
+            nc.sync.dma_start(out=out[t * P : (t + 1) * P, :], in_=results[t][:])
 
-        def store_tile(t, n):
-            c = t // TILES_IN_CHUNK
-            rows = out[t * P : (t + 1) * P, n * HALF : (n + 1) * HALF]
-            nc.sync.dma_start(out=rows, in_=results[c, n][:, t % TILES_IN_CHUNK, :])
+        def store_half(t, n):
+            columns = slice(n * HALF, (n + 1) * HALF)
+            nc.sync.dma_start(out=out[t * P : (t + 1) * P, columns], in_=results[t][:, columns])
 
         def last_half(t, n):
             h_codes, h_scales = h_mx[t]
-            for part, engine in enumerate((SCALAR, VECTOR)):
+            for part, engine in enumerate((VECTOR, SCALAR)):
                 bank = take_bank((t, n, part), f"last{part}", [P, WIDTH])
                 for s in range(WIDTH // P):
                     first = n * HALF + part * WIDTH + s * P
@@ -264,132 +278,100 @@ def tile_mix_lowrank_tm_none_kernel(tc, x, w4_words, w4_scales, down, up, out):
 
         nc.vector.memset(w4_planes[:].rearrange("p g n -> p (g n)").bitcast(I32), 0)
 
-        load_x(0, 0)
-        load_x(0, 1)
-        load_down(0, 0, P)
+        load_x(0, 2, 0)
         load_w4_scales()
         load_w4_codes()
-        load_down(1, 0, P // 2)
-        load_down(1, P // 2, P // 2)
-        for g in range(K_PASSES):
-            load_x(1, g)
-        load_up(0)
-        load_up(1)
-        for g in range(K_PASSES):
-            load_x(2, g)
-        load_up(2)
-        load_up(3)
-        for g in range(K_PASSES):
-            load_x(3, g)
+        load_x(0, 2, 1)
+        load_down(0, 0, P)
+        load_down(1, 0, P)
+        load_up(0, 2)
+        load_up(2, 2)
+        for c in (2, 3):
+            for g in range(K_PASSES):
+                load_x(c, 1, g)
 
         for g in range(K_PASSES):
             prepare_x(0, g, 96)
+            prepare_x(1, g, 96)
+            for t in range(4):
+                base(t, 0, g)
         interleave_down(0, 0, P, 44)
         quantise_down(0, 0, R)
-        for t in (0, 1):
-            for n in range(2):
-                for g in range(K_PASSES):
-                    base(t, n, g)
-        make_h(0, 0)
-        make_h(1, 0)
-        for first in (0, P // 2):
-            interleave_down(1, first, P // 2, 24)
-            for i in range(PACK):
-                quantise_down(1, i * P + first, P // 2)
-        make_h(0, 1)
-        make_h(1, 1)
-
-        prepare_x(1, 0, 96)
-        empty_h(0, SCALAR)
-        empty_h(1, SCALAR)
-        base(2, 0, 0)
-        base(3, 0, 0)
-        make_h(2, 0)
-        make_h(3, 0)
-        prepare_x(1, 1, between=0)
-        make_h(2, 1)
-        make_h(3, 1)
-        base(2, 0, 1)
-        base(3, 0, 1)
-        prepare_up(0, 96, between=1)
-        empty_h(2, SCALAR)
-        empty_h(3, SCALAR)
-        base(2, 1, 0)
-        base(2, 1, 1)
-        base(3, 1, 0)
-        prepare_up(1, between=2)
+        for t in range(4):
+            make_h(t, 0)
+        interleave_down(1, 0, P, 44)
+        for i in range(PACK):
+            quantise_down(1, i * P, P)
+        for t in range(4):
+            make_h(t, 1)
+            empty_h(t, SCALAR)
+        prepare_up(0, between=0)
         for t in range(3):
-            branch(t, 0)
-
-        prepare_x(2, 0, 96, between=3)
-        branch(3, 0)
+            for g in range(K_PASSES):
+                base(t, 1, g)
+        prepare_up(1, between=1)
+        quantise_h(2)
+        base(3, 1, 0)
         base(3, 1, 1)
+        quantise_h(3)
+        for t in range(4):
+            branch(t, 0)
+        interleave_up_shared()
         for t in range(4):
             empty(t, 0, SCALAR)
-        make_h(4, 0)
-        make_h(5, 0)
-        prepare_x(2, 1)
-        make_h(4, 1)
-        make_h(5, 1)
+        for t in range(4):
+            branch(t, 1)
+
+        prepare_x(2, 0)
+        for t in range(4):
+            empty(t, 1, SCALAR)
         for t in (4, 5):
-            for g in range(K_PASSES):
-                base(t, 0, g)
+            make_h(t, 0)
+        for n in range(2):
+            base(4, n, 0)
+        prepare_x(2, 1)
+        for t in (4, 5):
+            make_h(t, 1)
+        for n in range(2):
+            base(4, n, 1)
         empty_h(4, SCALAR)
         empty_h(5, SCALAR)
-        prepare_up(2)
-        prepare_up(3, between=4)
-        base(4, 1, 0)
-        base(4, 1, 1)
-        branch(4, 0)
-        branch(0, 1)
-        branch(1, 1)
-        prepare_x(3, 0, 96, between=5)
-        branch(2, 1)
-        branch(3, 1)
-        branch(5, 0)
-        branch(4, 1)
-        empty(4, 0, SCALAR)
-        empty(0, 1, SCALAR)
-        empty(1, 1, SCALAR)
-
+        prepare_x(3, 0)
+        for n in range(2):
+            for g in range(K_PASSES):
+                base(5, n, g)
+        prepare_x(3, 1, between=4)
         make_h(6, 0)
-        prepare_x(3, 1)
+        branch(4, 0)
+        branch(4, 1)
+        quantise_h(5)
         make_h(6, 1)
-        base(5, 1, 0)
-        base(5, 1, 1)
+        branch(5, 0)
         branch(5, 1)
-        empty(2, 1, SCALAR)
-        empty(3, 1, VECTOR)
-        empty(5, 0, SCALAR)
+        empty(4, 0, SCALAR)
+        empty(4, 1, VECTOR)
+        empty_h(6, SCALAR)
+        empty(5, 0, VECTOR)
         make_h(7, 0)
         make_h(7, 1)
-        empty_h(6, VECTOR)
-        base(6, 0, 0)
-        base(6, 0, 1)
         quantise_h(6)
-        branch(6, 0)
-        empty(4, 1, SCALAR)
-        base(6, 1, 0)
-        base(6, 1, 1)
         empty(5, 1, SCALAR)
         empty_h(7, VECTOR)
-        branch(6, 1)
+        for n in range(2):
+            for g in range(K_PASSES):
+                base(6, n, g)
+            branch(6, n)
         quantise_h(7)
+        empty(6, 0, SCALAR)
+        empty(6, 1, VECTOR)
         base(7, 0, 0)
         base(7, 0, 1)
         branch(7, 0)
-        empty(6, 0, SCALAR)
-        empty(6, 1, VECTOR)
-        empty(7, 0, VECTOR)
+        empty(7, 0, SCALAR)
 
-        store_chunk(0, 0)
-        store_chunk(1, 0)
-        store_tile(4, 0)
-        store_chunk(0, 1)
-        store_chunk(1, 1)
-        store_tile(5, 0)
-        store_chunk(2, 1)
-        store_tile(6, 0)
-        store_tile(6, 1)
-        store_tile(7, 0)
+        for t in range(6):
+            store_tile(t)
+        store_half(6, 0)
+        store_half(6, 1)
+        store_half(7, 0)
         last_half(7, 1)

@@ -65,50 +65,49 @@ def tile_mix_lowrank_tm_none_kernel(tc, x, w4_words, w4_scales, down, up, out):
                 raw.rearrange("p j (c i) -> p c j i", i=4),
             )
 
-        x_raw, x_mx = {}, {}
+        def prepare(strips, scalar_strips=0, between=()):
+            grouped = [sbuf(f"{name}_grouped", [P, P, PACK], BF16) for name, raw, codes, scales in strips]
+            own = len(strips) - scalar_strips
+            waiting = list(between)
 
-        def load_x(first, count, g):
-            raw = sbuf(f"x{first}{g}_raw", [P, PACK, count * WIDTH], F32)
-            rows = x[g * ROWS : (g + 1) * ROWS, first * WIDTH : (first + count) * WIDTH]
-            nc.sync.dma_start(out=raw[:], in_=rows.rearrange("(p j) t -> p j t", j=PACK))
-            for c in range(count):
-                x_raw[first + c, g] = raw[:, :, c * WIDTH : (c + 1) * WIDTH]
-
-        def prepare(name, raw, codes, scales, scalar_columns, between):
-            grouped = sbuf(f"{name}_grouped", [P, WIDTH, PACK], BF16)
-
-            def quantise_columns(first, count):
+            def quantise_strip(s):
+                name, raw, codes, scales = strips[s]
                 nc.vector.quantize_mx(
-                    out=codes[:, first : first + count].bitcast(E4M3),
-                    scales=scales[:, first : first + count],
-                    in_=grouped[:, first : first + count].rearrange("p c j -> p (c j)"),
+                    out=codes.bitcast(E4M3), scales=scales, in_=grouped[s][:].rearrange("p c j -> p (c j)")
                 )
 
-            if scalar_columns:
-                split = WIDTH - scalar_columns
-                interleave(VECTOR, grouped[:, :split], raw[:, :, :split])
-                interleave(SCALAR, grouped[:, split:], raw[:, :, split:])
-                if between is not None:
-                    quantise_h(between)
-                quantise_columns(0, WIDTH)
-            else:
-                interleave(VECTOR, grouped[:, :P], raw[:, :, :P])
-                interleave(VECTOR, grouped[:, P:], raw[:, :, P:])
-                quantise_columns(0, P)
-                if between is not None:
-                    quantise_h(between)
-                quantise_columns(P, P)
+            for s in range(own, len(strips)):
+                interleave(SCALAR, grouped[s][:], strips[s][1])
+            for s in range(own):
+                interleave(VECTOR, grouped[s][:], strips[s][1])
+                if s > 0:
+                    quantise_strip(s - 1)
+            for s in range(own - 1, len(strips)):
+                if waiting:
+                    quantise_h(waiting[0])
+                    waiting.remove(waiting[0])
+                quantise_strip(s)
+            for t in waiting:
+                quantise_h(t)
 
-        def prepare_x(c, g, scalar_columns=0, between=None):
-            codes = sbuf(f"x{c}{g}_codes", [P, WIDTH], U32)
-            scales = sbuf(f"x{c}{g}_scales", [P, WIDTH], U8)
-            x_mx[c, g] = codes, scales
-            prepare(f"x{c}{g}", x_raw[c, g], codes[:], scales[:], scalar_columns, between)
+        x_raw, x_mx = {}, {}
+
+        def load_x(tiles, g):
+            raw = sbuf(f"x{tiles[0]}{g}_raw", [P, PACK, len(tiles) * P], F32)
+            rows = x[g * ROWS : (g + 1) * ROWS, tiles[0] * P : (tiles[-1] + 1) * P]
+            nc.sync.dma_start(out=raw[:], in_=rows.rearrange("(p j) t -> p j t", j=PACK))
+            for s, t in enumerate(tiles):
+                x_raw[t, g] = raw[:, :, s * P : (s + 1) * P]
+
+        def prepare_x(tiles, g, scalar_strips=0, between=()):
+            for t in tiles:
+                x_mx[t, g] = sbuf(f"x{t}{g}_codes", [P, P], U32), sbuf(f"x{t}{g}_scales", [P, P], U8)
+            strips = [(f"x{t}{g}", x_raw[t, g], x_mx[t, g][0][:], x_mx[t, g][1][:]) for t in tiles]
+            prepare(strips, scalar_strips, between)
 
         def x_tile(t, g):
-            codes, scales = x_mx[t // TILES_IN_CHUNK, g]
-            first = (t % TILES_IN_CHUNK) * P
-            return codes[:, first : first + P].bitcast(E4M3), scales[:, first : first + P]
+            codes, scales = x_mx[t, g]
+            return codes[:].bitcast(E4M3), scales[:]
 
         down_raw = {}
         down_grouped = [sbuf(f"down{g}_grouped", [P, PACK, P, PACK], BF16) for g in range(K_PASSES)]
@@ -121,8 +120,8 @@ def tile_mix_lowrank_tm_none_kernel(tc, x, w4_words, w4_scales, down, up, out):
             nc.sync.dma_start(out=down_raw[g, first][:], in_=rows.rearrange("(p j) r -> p j r", j=PACK))
 
         def interleave_down(g, first, count, scalar_count):
-            grouped = down_grouped[g][:].rearrange("p i m j -> p m i j")[:, first : first + count]
-            raw = down_raw[g, first][:].rearrange("p j (m i) -> p m i j", i=PACK)
+            grouped = down_grouped[g][:].rearrange("p i m j -> p m j i")[:, first : first + count]
+            raw = down_raw[g, first][:].rearrange("p j (m i) -> p m j i", i=PACK)
             split = count - scalar_count
             copy(VECTOR, grouped[:, :split], raw[:, :split])
             if scalar_count:
@@ -140,27 +139,27 @@ def tile_mix_lowrank_tm_none_kernel(tc, x, w4_words, w4_scales, down, up, out):
         up_codes = [sbuf(f"up{n}_codes", [P, HALF], U32) for n in range(2)]
         up_scales = [sbuf(f"up{n}_scales", [P, HALF], U8) for n in range(2)]
 
-        def load_up(first, count):
-            raw = sbuf(f"up{first}_raw", [P, PACK, count * WIDTH], F32)
-            rows = up[:, first * WIDTH : (first + count) * WIDTH]
-            nc.sync.dma_start(out=raw[:], in_=rows.rearrange("(p j) n -> p j n", j=PACK))
-            for q in range(count):
-                up_raw[first + q] = raw[:, :, q * WIDTH : (q + 1) * WIDTH]
+        def load_up(n):
+            up_raw[n] = sbuf(f"up{n}_raw", [P, PACK, HALF], F32)
+            rows = up[:, n * HALF : (n + 1) * HALF]
+            nc.sync.dma_start(out=up_raw[n][:], in_=rows.rearrange("(p j) n -> p j n", j=PACK))
 
-        def prepare_up(q, scalar_columns=0, between=None):
-            n, columns = q // 2, slice((q % 2) * WIDTH, (q % 2 + 1) * WIDTH)
-            prepare(f"up{q}", up_raw[q], up_codes[n][:, columns], up_scales[n][:, columns], scalar_columns, between)
+        def prepare_up(n, scalar_strips=0, between=()):
+            columns = [slice(first, first + P) for first in range(0, HALF, P)]
+            strips = [(f"up{n}{c.start}", up_raw[n][:, :, c], up_codes[n][:, c], up_scales[n][:, c]) for c in columns]
+            prepare(strips, scalar_strips, between)
 
-        def interleave_up_shared():
-            grouped = sbuf("up_right_grouped", [P, HALF, PACK], BF16)
-            split = 64
-            interleave(VECTOR, grouped[:, :WIDTH], up_raw[2])
-            interleave(VECTOR, grouped[:, WIDTH : WIDTH + split], up_raw[3][:, :, :split])
-            interleave(SCALAR, grouped[:, WIDTH + split :], up_raw[3][:, :, split:])
+        def prepare_up_shared(n, scalar_columns, between):
+            grouped = sbuf(f"up{n}_grouped", [P, HALF, PACK], BF16)
+            split = HALF - scalar_columns
+            interleave(SCALAR, grouped[:, split:], up_raw[n][:, :, split:])
+            interleave(VECTOR, grouped[:, :WIDTH], up_raw[n][:, :, :WIDTH])
+            interleave(VECTOR, grouped[:, WIDTH:split], up_raw[n][:, :, WIDTH:split])
+            quantise_h(between)
             for first in (0, WIDTH):
                 nc.vector.quantize_mx(
-                    out=up_codes[1][:, first : first + WIDTH].bitcast(E4M3),
-                    scales=up_scales[1][:, first : first + WIDTH],
+                    out=up_codes[n][:, first : first + WIDTH].bitcast(E4M3),
+                    scales=up_scales[n][:, first : first + WIDTH],
                     in_=grouped[:, first : first + WIDTH].rearrange("p c j -> p (c j)"),
                 )
 
@@ -230,126 +229,125 @@ def tile_mix_lowrank_tm_none_kernel(tc, x, w4_words, w4_scales, down, up, out):
                 stop=True,
             )
 
-        results = {}
+        results = sbuf("results", [P, T // P, N], F32)
 
         def empty(t, n, engine):
-            if t not in results:
-                results[t] = sbuf(f"result{t}", [P, N], F32)
-            copy(engine, results[t][:, n * HALF : (n + 1) * HALF], sums[t, n][:])
+            copy(engine, results[:, t, n * HALF : (n + 1) * HALF], sums[t, n][:])
             give_back((t, n))
 
-        def store_tile(t):
-            nc.sync.dma_start(out=out[t * P : (t + 1) * P, :], in_=results[t][:])
+        def store(tiles, halves):
+            columns = slice(halves[0] * HALF, (halves[-1] + 1) * HALF)
+            rows = out[tiles[0] * P : (tiles[-1] + 1) * P, columns]
+            nc.sync.dma_start(
+                out=rows.rearrange("(t p) n -> p t n", p=P), in_=results[:, tiles[0] : tiles[-1] + 1, columns]
+            )
 
-        def store_half(t, n):
-            columns = slice(n * HALF, (n + 1) * HALF)
-            nc.sync.dma_start(out=out[t * P : (t + 1) * P, columns], in_=results[t][:, columns])
-
-        def last_half(t, n):
+        def quarter(t, q, engine):
             h_codes, h_scales = h_mx[t]
-            for part, engine in enumerate((VECTOR, SCALAR)):
-                bank = take_bank((t, n, part), f"last{part}", [P, WIDTH])
-                for s in range(WIDTH // P):
-                    first = n * HALF + part * WIDTH + s * P
-                    for g in range(K_PASSES):
-                        codes, scales = x_tile(t, g)
-                        nc.tensor.matmul_mx(
-                            out=bank[:, s * P : (s + 1) * P],
-                            lhsT=codes,
-                            lhsT_scale=scales,
-                            rhs=w4_codes[:, g, 2 * first : 2 * (first + P)].bitcast(E2M1),
-                            rhs_scale=w4_planes[:, g, first : first + P],
-                            start=(g == 0 and s == 0),
-                            stop=False,
-                        )
-                nc.tensor.matmul_mx(
-                    out=bank[:],
-                    lhsT=h_codes[:].bitcast(E4M3),
-                    lhsT_scale=h_scales[:],
-                    rhs=up_codes[n][:, part * WIDTH : (part + 1) * WIDTH].bitcast(E4M3),
-                    rhs_scale=up_scales[n][:, part * WIDTH : (part + 1) * WIDTH],
-                    start=False,
-                    stop=True,
-                )
-                result = sbuf(f"last{part}_result", [P, WIDTH], F32)
-                copy(engine, result[:], bank[:])
-                first = n * HALF + part * WIDTH
-                nc.sync.dma_start(out=out[t * P : (t + 1) * P, first : first + WIDTH], in_=result[:])
+            n, part = divmod(q, 2)
+            bank = take_bank((t, "quarter", q), f"quarter{q}", [P, WIDTH])
+            for s in range(WIDTH // P):
+                first = q * WIDTH + s * P
+                for g in range(K_PASSES):
+                    codes, scales = x_tile(t, g)
+                    nc.tensor.matmul_mx(
+                        out=bank[:, s * P : (s + 1) * P],
+                        lhsT=codes,
+                        lhsT_scale=scales,
+                        rhs=w4_codes[:, g, 2 * first : 2 * (first + P)].bitcast(E2M1),
+                        rhs_scale=w4_planes[:, g, first : first + P],
+                        start=(g == 0 and s == 0),
+                        stop=False,
+                    )
+            nc.tensor.matmul_mx(
+                out=bank[:],
+                lhsT=h_codes[:].bitcast(E4M3),
+                lhsT_scale=h_scales[:],
+                rhs=up_codes[n][:, part * WIDTH : (part + 1) * WIDTH].bitcast(E4M3),
+                rhs_scale=up_scales[n][:, part * WIDTH : (part + 1) * WIDTH],
+                start=False,
+                stop=True,
+            )
+            result = sbuf(f"quarter{q}_result", [P, WIDTH], F32)
+            copy(engine, result[:], bank[:])
+            nc.sync.dma_start(out=out[t * P : (t + 1) * P, q * WIDTH : (q + 1) * WIDTH], in_=result[:])
 
         nc.vector.memset(w4_planes[:].rearrange("p g n -> p (g n)").bitcast(I32), 0)
 
-        load_x(0, 2, 0)
+        FIRST, SECOND, THIRD = (0, 1, 2, 3), (4, 5), (6, 7)
+        load_x(FIRST, 0)
         load_w4_scales()
         load_w4_codes()
-        load_x(0, 2, 1)
         load_down(0, 0, P)
+        load_x(FIRST, 1)
         load_down(1, 0, P)
-        load_up(0, 2)
-        load_up(2, 2)
-        for c in (2, 3):
+        load_up(0)
+        load_up(1)
+        for tiles in (SECOND, THIRD):
             for g in range(K_PASSES):
-                load_x(c, 1, g)
+                load_x(tiles, g)
 
-        for g in range(K_PASSES):
-            prepare_x(0, g, 96)
-            prepare_x(1, g, 96)
-            for t in range(4):
-                base(t, 0, g)
+        prepare_x(FIRST, 0, 1)
+        for t in FIRST:
+            base(t, 0, 0)
         interleave_down(0, 0, P, 44)
         quantise_down(0, 0, R)
-        for t in range(4):
+        for t in FIRST:
             make_h(t, 0)
+        prepare_x(FIRST, 1, 1)
+        for t in FIRST:
+            base(t, 0, 1)
         interleave_down(1, 0, P, 44)
         for i in range(PACK):
             quantise_down(1, i * P, P)
-        for t in range(4):
+        for t in FIRST:
             make_h(t, 1)
             empty_h(t, SCALAR)
-        prepare_up(0, between=0)
-        for t in range(3):
+        for t in FIRST[:-1]:
             for g in range(K_PASSES):
                 base(t, 1, g)
-        prepare_up(1, between=1)
-        quantise_h(2)
-        base(3, 1, 0)
-        base(3, 1, 1)
-        quantise_h(3)
-        for t in range(4):
+        prepare_up(0, 0, between=FIRST[:-1])
+        for t in FIRST[:-1]:
             branch(t, 0)
-        interleave_up_shared()
-        for t in range(4):
-            empty(t, 0, SCALAR)
-        for t in range(4):
+        for g in range(K_PASSES):
+            base(3, 1, g)
+        prepare_up_shared(1, 192, 3)
+        branch(3, 0)
+        for t in FIRST:
             branch(t, 1)
-
-        prepare_x(2, 0)
-        for t in range(4):
-            empty(t, 1, SCALAR)
-        for t in (4, 5):
+        prepare_x(SECOND, 0)
+        for n in range(2):
+            for t in FIRST[:-1]:
+                empty(t, n, SCALAR)
+        for t in SECOND:
             make_h(t, 0)
         for n in range(2):
             base(4, n, 0)
-        prepare_x(2, 1)
-        for t in (4, 5):
+        prepare_x(SECOND, 1)
+        for t in SECOND:
             make_h(t, 1)
         for n in range(2):
             base(4, n, 1)
+        empty(3, 0, SCALAR)
         empty_h(4, SCALAR)
+        empty(3, 1, SCALAR)
         empty_h(5, SCALAR)
-        prepare_x(3, 0)
-        for n in range(2):
-            for g in range(K_PASSES):
-                base(5, n, g)
-        prepare_x(3, 1, between=4)
-        make_h(6, 0)
+        prepare_x(THIRD, 0)
+        quantise_h(4)
+        for g in range(K_PASSES):
+            base(5, 0, g)
         branch(4, 0)
         branch(4, 1)
+        for g in range(K_PASSES):
+            base(5, 1, g)
+        prepare_x(THIRD, 1)
         quantise_h(5)
+        empty(4, 0, SCALAR)
+        empty(4, 1, VECTOR)
+        make_h(6, 0)
         make_h(6, 1)
         branch(5, 0)
         branch(5, 1)
-        empty(4, 0, SCALAR)
-        empty(4, 1, VECTOR)
         empty_h(6, SCALAR)
         empty(5, 0, VECTOR)
         make_h(7, 0)
@@ -364,14 +362,11 @@ def tile_mix_lowrank_tm_none_kernel(tc, x, w4_words, w4_scales, down, up, out):
         quantise_h(7)
         empty(6, 0, SCALAR)
         empty(6, 1, VECTOR)
-        base(7, 0, 0)
-        base(7, 0, 1)
-        branch(7, 0)
-        empty(7, 0, SCALAR)
+
 
         for t in range(6):
-            store_tile(t)
-        store_half(6, 0)
-        store_half(6, 1)
-        store_half(7, 0)
-        last_half(7, 1)
+            store((t,), (0, 1))
+        store((6,), (0,))
+        store((6,), (1,))
+        for q in range(4):
+            quarter(7, q, VECTOR if q % 2 else SCALAR)

@@ -16,11 +16,15 @@ E2M1 = mybir.dt.float4_e2m1fn_x4
 P = 128
 PACK = 4
 ROWS = P * PACK
-K_PASSES = K // ROWS
-WIDTH = 256
-TILES_IN_CHUNK = WIDTH // P
+PASSES = range(K // ROWS)
 HALF = 512
+HALVES = range(N // HALF)
 BANKS = 8
+
+FIRST, SECOND, THIRD = (0, 1, 2, 3), (4, 5), (6, 7)
+
+DOWN_SCALAR_SHARE = 44
+UP_SCALAR_SHARE = 192
 
 
 def tile_mix_lowrank_tm_none_kernel(tc, x, w4_words, w4_scales, down, up, out):
@@ -52,12 +56,6 @@ def tile_mix_lowrank_tm_none_kernel(tc, x, w4_words, w4_scales, down, up, out):
             else:
                 nc.vector.tensor_copy(out=dst, in_=src)
 
-        def quantise(name, width, grouped):
-            codes = sbuf(f"{name}_codes", [P, width], U32)
-            scales = sbuf(f"{name}_scales", [P, width], U8)
-            nc.vector.quantize_mx(out=codes[:].bitcast(E4M3), scales=scales[:], in_=grouped)
-            return codes, scales
-
         def interleave(engine, grouped, raw):
             copy(
                 engine,
@@ -65,16 +63,16 @@ def tile_mix_lowrank_tm_none_kernel(tc, x, w4_words, w4_scales, down, up, out):
                 raw.rearrange("p j (c i) -> p c j i", i=4),
             )
 
-        def prepare(strips, scalar_strips=0, between=()):
+        def quantise(codes, scales, grouped):
+            nc.vector.quantize_mx(out=codes.bitcast(E4M3), scales=scales, in_=grouped.rearrange("p c j -> p (c j)"))
+
+        def prepare(strips, scalar_strips, h_tiles):
             grouped = [sbuf(f"{name}_grouped", [P, P, PACK], BF16) for name, raw, codes, scales in strips]
             own = len(strips) - scalar_strips
-            waiting = list(between)
 
             def quantise_strip(s):
                 name, raw, codes, scales = strips[s]
-                nc.vector.quantize_mx(
-                    out=codes.bitcast(E4M3), scales=scales, in_=grouped[s][:].rearrange("p c j -> p (c j)")
-                )
+                quantise(codes, scales, grouped[s][:])
 
             for s in range(own, len(strips)):
                 interleave(SCALAR, grouped[s][:], strips[s][1])
@@ -82,12 +80,11 @@ def tile_mix_lowrank_tm_none_kernel(tc, x, w4_words, w4_scales, down, up, out):
                 interleave(VECTOR, grouped[s][:], strips[s][1])
                 if s > 0:
                     quantise_strip(s - 1)
+            for t in h_tiles[:1]:
+                quantise_h(t)
             for s in range(own - 1, len(strips)):
-                if waiting:
-                    quantise_h(waiting[0])
-                    waiting.remove(waiting[0])
                 quantise_strip(s)
-            for t in waiting:
+            for t in h_tiles[1:]:
                 quantise_h(t)
 
         x_raw, x_mx = {}, {}
@@ -99,98 +96,82 @@ def tile_mix_lowrank_tm_none_kernel(tc, x, w4_words, w4_scales, down, up, out):
             for s, t in enumerate(tiles):
                 x_raw[t, g] = raw[:, :, s * P : (s + 1) * P]
 
-        def prepare_x(tiles, g, scalar_strips=0, between=()):
+        def prepare_x(tiles, g, scalar_strips=0):
             for t in tiles:
                 x_mx[t, g] = sbuf(f"x{t}{g}_codes", [P, P], U32), sbuf(f"x{t}{g}_scales", [P, P], U8)
             strips = [(f"x{t}{g}", x_raw[t, g], x_mx[t, g][0][:], x_mx[t, g][1][:]) for t in tiles]
-            prepare(strips, scalar_strips, between)
-
-        def x_tile(t, g):
-            codes, scales = x_mx[t, g]
-            return codes[:].bitcast(E4M3), scales[:]
+            prepare(strips, scalar_strips, ())
 
         down_raw = {}
-        down_grouped = [sbuf(f"down{g}_grouped", [P, PACK, P, PACK], BF16) for g in range(K_PASSES)]
-        down_codes = [sbuf(f"down{g}_codes", [P, R], U32) for g in range(K_PASSES)]
-        down_scales = [sbuf(f"down{g}_scales", [P, R], U8) for g in range(K_PASSES)]
+        down_grouped = [sbuf(f"down{g}_grouped", [P, R, PACK], BF16) for g in PASSES]
+        down_codes = [sbuf(f"down{g}_codes", [P, R], U32) for g in PASSES]
+        down_scales = [sbuf(f"down{g}_scales", [P, R], U8) for g in PASSES]
 
-        def load_down(g, first, count):
-            down_raw[g, first] = sbuf(f"down{g}{first}_raw", [P, PACK, PACK * count], F32)
-            rows = down[g * ROWS : (g + 1) * ROWS, PACK * first : PACK * (first + count)]
-            nc.sync.dma_start(out=down_raw[g, first][:], in_=rows.rearrange("(p j) r -> p j r", j=PACK))
+        def load_down(g):
+            down_raw[g] = sbuf(f"down{g}_raw", [P, PACK, R], F32)
+            rows = down[g * ROWS : (g + 1) * ROWS, :]
+            nc.sync.dma_start(out=down_raw[g][:], in_=rows.rearrange("(p j) r -> p j r", j=PACK))
 
-        def interleave_down(g, first, count, scalar_count):
-            grouped = down_grouped[g][:].rearrange("p i m j -> p m j i")[:, first : first + count]
-            raw = down_raw[g, first][:].rearrange("p j (m i) -> p m j i", i=PACK)
-            split = count - scalar_count
+        def prepare_down(g, width):
+            grouped = down_grouped[g][:].rearrange("p (i m) j -> p m j i", i=PACK)
+            raw = down_raw[g][:].rearrange("p j (m i) -> p m j i", i=PACK)
+            split = P - DOWN_SCALAR_SHARE
             copy(VECTOR, grouped[:, :split], raw[:, :split])
-            if scalar_count:
-                copy(SCALAR, grouped[:, split:], raw[:, split:])
-
-        def quantise_down(g, first, count):
-            grouped = down_grouped[g][:].rearrange("p i m j -> p (i m j)")
-            nc.vector.quantize_mx(
-                out=down_codes[g][:, first : first + count].bitcast(E4M3),
-                scales=down_scales[g][:, first : first + count],
-                in_=grouped[:, PACK * first : PACK * (first + count)],
-            )
+            copy(SCALAR, grouped[:, split:], raw[:, split:])
+            for first in range(0, R, width):
+                columns = slice(first, first + width)
+                quantise(down_codes[g][:, columns], down_scales[g][:, columns], down_grouped[g][:, columns])
 
         up_raw = {}
-        up_codes = [sbuf(f"up{n}_codes", [P, HALF], U32) for n in range(2)]
-        up_scales = [sbuf(f"up{n}_scales", [P, HALF], U8) for n in range(2)]
+        up_codes = [sbuf(f"up{n}_codes", [P, HALF], U32) for n in HALVES]
+        up_scales = [sbuf(f"up{n}_scales", [P, HALF], U8) for n in HALVES]
 
         def load_up(n):
             up_raw[n] = sbuf(f"up{n}_raw", [P, PACK, HALF], F32)
             rows = up[:, n * HALF : (n + 1) * HALF]
             nc.sync.dma_start(out=up_raw[n][:], in_=rows.rearrange("(p j) n -> p j n", j=PACK))
 
-        def prepare_up(n, scalar_strips=0, between=()):
+        def prepare_up_alone(n, h_tiles):
             columns = [slice(first, first + P) for first in range(0, HALF, P)]
             strips = [(f"up{n}{c.start}", up_raw[n][:, :, c], up_codes[n][:, c], up_scales[n][:, c]) for c in columns]
-            prepare(strips, scalar_strips, between)
+            prepare(strips, 0, h_tiles)
 
-        def prepare_up_shared(n, scalar_columns, between):
+        def prepare_up_shared(n, h_tile):
             grouped = sbuf(f"up{n}_grouped", [P, HALF, PACK], BF16)
-            split = HALF - scalar_columns
+            middle, split = HALF // 2, HALF - UP_SCALAR_SHARE
             interleave(SCALAR, grouped[:, split:], up_raw[n][:, :, split:])
-            interleave(VECTOR, grouped[:, :WIDTH], up_raw[n][:, :, :WIDTH])
-            interleave(VECTOR, grouped[:, WIDTH:split], up_raw[n][:, :, WIDTH:split])
-            quantise_h(between)
-            for first in (0, WIDTH):
-                nc.vector.quantize_mx(
-                    out=up_codes[n][:, first : first + WIDTH].bitcast(E4M3),
-                    scales=up_scales[n][:, first : first + WIDTH],
-                    in_=grouped[:, first : first + WIDTH].rearrange("p c j -> p (c j)"),
-                )
+            interleave(VECTOR, grouped[:, :middle], up_raw[n][:, :, :middle])
+            interleave(VECTOR, grouped[:, middle:split], up_raw[n][:, :, middle:split])
+            quantise_h(h_tile)
+            for columns in (slice(0, middle), slice(middle, HALF)):
+                quantise(up_codes[n][:, columns], up_scales[n][:, columns], grouped[:, columns])
 
-        w4_codes = sbuf("w4_codes", [P, K_PASSES, 2 * N], U8)
-        w4_planes = sbuf("w4_planes", [P, K_PASSES, N], U8)
+        w4_codes = sbuf("w4_codes", [P, len(PASSES), 2 * N], U8)
+        w4_scale_rows = sbuf("w4_scale_rows", [P, len(PASSES), N], U8)
 
-        def load_w4_scales():
+        def load_w4():
             for quadrant in range(4):
                 nc.sync.dma_start(
-                    out=w4_planes[32 * quadrant : 32 * quadrant + 4].bitcast(I32),
+                    out=w4_scale_rows[32 * quadrant : 32 * quadrant + 4].bitcast(I32),
                     in_=w4_scales[:, 4 * quadrant : 4 * quadrant + 4, :].rearrange("g s n -> s g n").bitcast(I32),
                 )
-
-        def load_w4_codes():
             nc.sync.dma_start(out=w4_codes[:].bitcast(I32), in_=w4_words.rearrange("g p n -> p g n").bitcast(I32))
 
         h_sums, h_grouped, h_mx = {}, {}, {}
 
         def make_h(t, g):
-            if g == 0:
+            if g == PASSES[0]:
                 h_sums[t] = take_bank(("h", t), f"h{t}_sums", [P, PACK, P])
-            codes, scales = x_tile(t, g)
+            codes, scales = x_mx[t, g]
             for i in range(PACK):
                 nc.tensor.matmul_mx(
                     out=h_sums[t][:, i, :],
                     lhsT=down_codes[g][:, i * P : (i + 1) * P].bitcast(E4M3),
                     lhsT_scale=down_scales[g][:, i * P : (i + 1) * P],
-                    rhs=codes,
-                    rhs_scale=scales,
-                    start=(g == 0 and i == 0),
-                    stop=(g == K_PASSES - 1 and i == PACK - 1),
+                    rhs=codes[:].bitcast(E4M3),
+                    rhs_scale=scales[:],
+                    start=(g == PASSES[0] and i == 0),
+                    stop=(g == PASSES[-1] and i == PACK - 1),
                 )
 
         def empty_h(t, engine):
@@ -199,23 +180,26 @@ def tile_mix_lowrank_tm_none_kernel(tc, x, w4_words, w4_scales, down, up, out):
             give_back(("h", t))
 
         def quantise_h(t):
-            h_mx[t] = quantise(f"h{t}", P, h_grouped[t][:].rearrange("p t i -> p (t i)"))
+            h_mx[t] = sbuf(f"h{t}_codes", [P, P], U32), sbuf(f"h{t}_scales", [P, P], U8)
+            quantise(h_mx[t][0][:], h_mx[t][1][:], h_grouped[t][:])
 
         sums = {}
+        results = sbuf("results", [P, T // P, N], F32)
 
-        def base(t, n, g):
-            if g == 0:
-                sums[t, n] = take_bank((t, n), f"sums{t}{n}", [P, HALF])
-            codes, scales = x_tile(t, g)
-            nc.tensor.matmul_mx(
-                out=sums[t, n][:],
-                lhsT=codes,
-                lhsT_scale=scales,
-                rhs=w4_codes[:, g, 2 * HALF * n : 2 * HALF * (n + 1)].bitcast(E2M1),
-                rhs_scale=w4_planes[:, g, HALF * n : HALF * (n + 1)],
-                start=(g == 0),
-                stop=False,
-            )
+        def base(t, n, passes=PASSES):
+            for g in passes:
+                if g == PASSES[0]:
+                    sums[t, n] = take_bank((t, n), f"sums{t}{n}", [P, HALF])
+                codes, scales = x_mx[t, g]
+                nc.tensor.matmul_mx(
+                    out=sums[t, n][:],
+                    lhsT=codes[:].bitcast(E4M3),
+                    lhsT_scale=scales[:],
+                    rhs=w4_codes[:, g, 2 * HALF * n : 2 * HALF * (n + 1)].bitcast(E2M1),
+                    rhs_scale=w4_scale_rows[:, g, HALF * n : HALF * (n + 1)],
+                    start=(g == PASSES[0]),
+                    stop=False,
+                )
 
         def branch(t, n):
             codes, scales = h_mx[t]
@@ -229,144 +213,102 @@ def tile_mix_lowrank_tm_none_kernel(tc, x, w4_words, w4_scales, down, up, out):
                 stop=True,
             )
 
-        results = sbuf("results", [P, T // P, N], F32)
-
         def empty(t, n, engine):
             copy(engine, results[:, t, n * HALF : (n + 1) * HALF], sums[t, n][:])
             give_back((t, n))
 
-        def store(tiles, halves):
-            columns = slice(halves[0] * HALF, (halves[-1] + 1) * HALF)
-            rows = out[tiles[0] * P : (tiles[-1] + 1) * P, columns]
+        def store(t, first, width):
             nc.sync.dma_start(
-                out=rows.rearrange("(t p) n -> p t n", p=P), in_=results[:, tiles[0] : tiles[-1] + 1, columns]
+                out=out[t * P : (t + 1) * P, first : first + width], in_=results[:, t, first : first + width]
             )
 
-        def quarter(t, q, engine):
-            h_codes, h_scales = h_mx[t]
-            n, part = divmod(q, 2)
-            bank = take_bank((t, "quarter", q), f"quarter{q}", [P, WIDTH])
-            for s in range(WIDTH // P):
-                first = q * WIDTH + s * P
-                for g in range(K_PASSES):
-                    codes, scales = x_tile(t, g)
-                    nc.tensor.matmul_mx(
-                        out=bank[:, s * P : (s + 1) * P],
-                        lhsT=codes,
-                        lhsT_scale=scales,
-                        rhs=w4_codes[:, g, 2 * first : 2 * (first + P)].bitcast(E2M1),
-                        rhs_scale=w4_planes[:, g, first : first + P],
-                        start=(g == 0 and s == 0),
-                        stop=False,
-                    )
-            nc.tensor.matmul_mx(
-                out=bank[:],
-                lhsT=h_codes[:].bitcast(E4M3),
-                lhsT_scale=h_scales[:],
-                rhs=up_codes[n][:, part * WIDTH : (part + 1) * WIDTH].bitcast(E4M3),
-                rhs_scale=up_scales[n][:, part * WIDTH : (part + 1) * WIDTH],
-                start=False,
-                stop=True,
-            )
-            result = sbuf(f"quarter{q}_result", [P, WIDTH], F32)
-            copy(engine, result[:], bank[:])
-            nc.sync.dma_start(out=out[t * P : (t + 1) * P, q * WIDTH : (q + 1) * WIDTH], in_=result[:])
+        nc.vector.memset(w4_scale_rows[:].rearrange("p g n -> p (g n)").bitcast(I32), 0)
 
-        nc.vector.memset(w4_planes[:].rearrange("p g n -> p (g n)").bitcast(I32), 0)
-
-        FIRST, SECOND, THIRD = (0, 1, 2, 3), (4, 5), (6, 7)
         load_x(FIRST, 0)
-        load_w4_scales()
-        load_w4_codes()
-        load_down(0, 0, P)
+        load_w4()
+        load_down(0)
         load_x(FIRST, 1)
-        load_down(1, 0, P)
-        load_up(0)
-        load_up(1)
+        load_down(1)
+        for n in HALVES:
+            load_up(n)
         for tiles in (SECOND, THIRD):
-            for g in range(K_PASSES):
+            for g in PASSES:
                 load_x(tiles, g)
 
-        prepare_x(FIRST, 0, 1)
+
+        prepare_x(FIRST, 0, scalar_strips=1)
         for t in FIRST:
-            base(t, 0, 0)
-        interleave_down(0, 0, P, 44)
-        quantise_down(0, 0, R)
+            base(t, 0, [0])
+        prepare_down(0, R)
         for t in FIRST:
             make_h(t, 0)
-        prepare_x(FIRST, 1, 1)
+        prepare_x(FIRST, 1, scalar_strips=1)
         for t in FIRST:
-            base(t, 0, 1)
-        interleave_down(1, 0, P, 44)
-        for i in range(PACK):
-            quantise_down(1, i * P, P)
+            base(t, 0, [1])
+        prepare_down(1, P)
         for t in FIRST:
             make_h(t, 1)
             empty_h(t, SCALAR)
-        for t in FIRST[:-1]:
-            for g in range(K_PASSES):
-                base(t, 1, g)
-        prepare_up(0, 0, between=FIRST[:-1])
-        for t in FIRST[:-1]:
+
+        leading, trailing = FIRST[:-1], FIRST[-1]
+        for t in leading:
+            base(t, 1)
+        prepare_up_alone(0, leading)
+        for t in leading:
             branch(t, 0)
-        for g in range(K_PASSES):
-            base(3, 1, g)
-        prepare_up_shared(1, 192, 3)
-        branch(3, 0)
+        base(trailing, 1)
+        prepare_up_shared(1, trailing)
+        branch(trailing, 0)
         for t in FIRST:
             branch(t, 1)
+
+        a, b = SECOND
         prepare_x(SECOND, 0)
-        for n in range(2):
-            for t in FIRST[:-1]:
+        for n in HALVES:
+            for t in leading:
                 empty(t, n, SCALAR)
-        for t in SECOND:
-            make_h(t, 0)
-        for n in range(2):
-            base(4, n, 0)
-        prepare_x(SECOND, 1)
-        for t in SECOND:
-            make_h(t, 1)
-        for n in range(2):
-            base(4, n, 1)
-        empty(3, 0, SCALAR)
-        empty_h(4, SCALAR)
-        empty(3, 1, SCALAR)
-        empty_h(5, SCALAR)
+        for g in PASSES:
+            if g > 0:
+                prepare_x(SECOND, g)
+            for t in SECOND:
+                make_h(t, g)
+            for n in HALVES:
+                base(a, n, [g])
+        for n, t in enumerate(SECOND):
+            empty(trailing, n, SCALAR)
+            empty_h(t, SCALAR)
         prepare_x(THIRD, 0)
-        quantise_h(4)
-        for g in range(K_PASSES):
-            base(5, 0, g)
-        branch(4, 0)
-        branch(4, 1)
-        for g in range(K_PASSES):
-            base(5, 1, g)
+        quantise_h(a)
+        base(b, 0)
+        for n in HALVES:
+            branch(a, n)
+        base(b, 1)
+
+        c, d = THIRD
         prepare_x(THIRD, 1)
-        quantise_h(5)
-        empty(4, 0, SCALAR)
-        empty(4, 1, VECTOR)
-        make_h(6, 0)
-        make_h(6, 1)
-        branch(5, 0)
-        branch(5, 1)
-        empty_h(6, SCALAR)
-        empty(5, 0, VECTOR)
-        make_h(7, 0)
-        make_h(7, 1)
-        quantise_h(6)
-        empty(5, 1, SCALAR)
-        empty_h(7, VECTOR)
-        for n in range(2):
-            for g in range(K_PASSES):
-                base(6, n, g)
-            branch(6, n)
-        quantise_h(7)
-        empty(6, 0, SCALAR)
-        empty(6, 1, VECTOR)
+        quantise_h(b)
+        empty(a, 0, SCALAR)
+        empty(a, 1, VECTOR)
+        for g in PASSES:
+            make_h(c, g)
+        for n in HALVES:
+            branch(b, n)
+        empty_h(c, SCALAR)
+        empty(b, 0, VECTOR)
+        for g in PASSES:
+            make_h(d, g)
+        quantise_h(c)
+        empty(b, 1, SCALAR)
+        empty_h(d, VECTOR)
+        quantise_h(d)
+        for t in THIRD:
+            for n in HALVES:
+                base(t, n)
+                branch(t, n)
+                empty(t, n, VECTOR if n else SCALAR)
 
-
-        for t in range(6):
-            store((t,), (0, 1))
-        store((6,), (0,))
-        store((6,), (1,))
-        for q in range(4):
-            quarter(7, q, VECTOR if q % 2 else SCALAR)
+        for t in FIRST + SECOND:
+            store(t, 0, N)
+        for t in THIRD:
+            for n in HALVES:
+                store(t, n * HALF, HALF)

@@ -19,6 +19,7 @@ ROWS = P * PACK
 PASSES = range(K // ROWS)
 HALF = 512
 HALVES = range(N // HALF)
+QUARTER = 256
 BANKS = 8
 
 FIRST, SECOND, THIRD = (0, 1, 2, 3), (4, 5), (6, 7)
@@ -112,14 +113,14 @@ def tile_mix_lowrank_tm_none_kernel(tc, x, w4_words, w4_scales, down, up, out):
             rows = down[g * ROWS : (g + 1) * ROWS, :]
             nc.sync.dma_start(out=down_raw[g][:], in_=rows.rearrange("(p j) r -> p j r", j=PACK))
 
-        def prepare_down(g, width):
-            grouped = down_grouped[g][:].rearrange("p (i m) j -> p m j i", i=PACK)
-            raw = down_raw[g][:].rearrange("p j (m i) -> p m j i", i=PACK)
+        def prepare_down(g):
+            grouped = down_grouped[g][:].rearrange("p (i m) j -> p m i j", i=PACK)
+            raw = down_raw[g][:].rearrange("p j (m i) -> p m i j", i=PACK)
             split = P - DOWN_SCALAR_SHARE
             copy(VECTOR, grouped[:, :split], raw[:, :split])
             copy(SCALAR, grouped[:, split:], raw[:, split:])
-            for first in range(0, R, width):
-                columns = slice(first, first + width)
+            for first in range(0, R, P):
+                columns = slice(first, first + P)
                 quantise(down_codes[g][:, columns], down_scales[g][:, columns], down_grouped[g][:, columns])
 
         up_raw = {}
@@ -217,6 +218,35 @@ def tile_mix_lowrank_tm_none_kernel(tc, x, w4_words, w4_scales, down, up, out):
             copy(engine, results[:, t, n * HALF : (n + 1) * HALF], sums[t, n][:])
             give_back((t, n))
 
+        def quarter(t, first, engine):
+            n, inside = divmod(first, HALF)
+            bank = take_bank((t, "quarter", first), f"quarter{first}", [P, QUARTER])
+            for strip in range(0, QUARTER, P):
+                column = first + strip
+                for g in PASSES:
+                    codes, scales = x_mx[t, g]
+                    nc.tensor.matmul_mx(
+                        out=bank[:, strip : strip + P],
+                        lhsT=codes[:].bitcast(E4M3),
+                        lhsT_scale=scales[:],
+                        rhs=w4_codes[:, g, 2 * column : 2 * (column + P)].bitcast(E2M1),
+                        rhs_scale=w4_scale_rows[:, g, column : column + P],
+                        start=(strip == 0 and g == PASSES[0]),
+                        stop=False,
+                    )
+            codes, scales = h_mx[t]
+            nc.tensor.matmul_mx(
+                out=bank[:],
+                lhsT=codes[:].bitcast(E4M3),
+                lhsT_scale=scales[:],
+                rhs=up_codes[n][:, inside : inside + QUARTER].bitcast(E4M3),
+                rhs_scale=up_scales[n][:, inside : inside + QUARTER],
+                start=False,
+                stop=True,
+            )
+            copy(engine, results[:, t, first : first + QUARTER], bank[:])
+            store(t, first, QUARTER)
+
         def store(t, first, width):
             nc.sync.dma_start(
                 out=out[t * P : (t + 1) * P, first : first + width], in_=results[:, t, first : first + width]
@@ -226,9 +256,9 @@ def tile_mix_lowrank_tm_none_kernel(tc, x, w4_words, w4_scales, down, up, out):
 
         load_x(FIRST, 0)
         load_w4()
-        load_down(0)
         load_x(FIRST, 1)
-        load_down(1)
+        for g in PASSES:
+            load_down(g)
         for n in HALVES:
             load_up(n)
         for tiles in (SECOND, THIRD):
@@ -236,18 +266,15 @@ def tile_mix_lowrank_tm_none_kernel(tc, x, w4_words, w4_scales, down, up, out):
                 load_x(tiles, g)
 
 
-        prepare_x(FIRST, 0, scalar_strips=1)
+        for g in PASSES:
+            prepare_x(FIRST, g, scalar_strips=1)
+            for t in FIRST:
+                base(t, 0, [g])
+        for g in PASSES:
+            prepare_down(g)
+            for t in FIRST:
+                make_h(t, g)
         for t in FIRST:
-            base(t, 0, [0])
-        prepare_down(0, R)
-        for t in FIRST:
-            make_h(t, 0)
-        prepare_x(FIRST, 1, scalar_strips=1)
-        for t in FIRST:
-            base(t, 0, [1])
-        prepare_down(1, P)
-        for t in FIRST:
-            make_h(t, 1)
             empty_h(t, SCALAR)
 
         leading, trailing = FIRST[:-1], FIRST[-1]
@@ -279,10 +306,10 @@ def tile_mix_lowrank_tm_none_kernel(tc, x, w4_words, w4_scales, down, up, out):
             empty_h(t, SCALAR)
         prepare_x(THIRD, 0)
         quantise_h(a)
-        base(b, 0)
+        for n in HALVES:
+            base(b, n)
         for n in HALVES:
             branch(a, n)
-        base(b, 1)
 
         c, d = THIRD
         prepare_x(THIRD, 1)
@@ -301,14 +328,14 @@ def tile_mix_lowrank_tm_none_kernel(tc, x, w4_words, w4_scales, down, up, out):
         empty(b, 1, SCALAR)
         empty_h(d, VECTOR)
         quantise_h(d)
-        for t in THIRD:
-            for n in HALVES:
-                base(t, n)
-                branch(t, n)
-                empty(t, n, VECTOR if n else SCALAR)
+        for n in HALVES:
+            base(c, n)
+            branch(c, n)
+            empty(c, n, VECTOR if n else SCALAR)
 
         for t in FIRST + SECOND:
             store(t, 0, N)
-        for t in THIRD:
-            for n in HALVES:
-                store(t, n * HALF, HALF)
+        for n in HALVES:
+            store(c, n * HALF, HALF)
+        for q, first in enumerate(range(0, N, QUARTER)):
+            quarter(d, first, VECTOR if q % 2 else SCALAR)

@@ -25,7 +25,6 @@ BANKS = 8
 FIRST, SECOND, THIRD = (0, 1, 2, 3), (4, 5), (6, 7)
 
 DOWN_SCALAR_SHARE = 44
-UP_SCALAR_SHARE = 192
 
 
 def tile_mix_lowrank_tm_none_kernel(tc, x, w4_words, w4_scales, down, up, out):
@@ -67,27 +66,6 @@ def tile_mix_lowrank_tm_none_kernel(tc, x, w4_words, w4_scales, down, up, out):
         def quantise(codes, scales, grouped):
             nc.vector.quantize_mx(out=codes.bitcast(E4M3), scales=scales, in_=grouped.rearrange("p c j -> p (c j)"))
 
-        def prepare(strips, scalar_strips, h_tiles):
-            grouped = [sbuf(f"{name}_grouped", [P, P, PACK], BF16) for name, raw, codes, scales in strips]
-            own = len(strips) - scalar_strips
-
-            def quantise_strip(s):
-                name, raw, codes, scales = strips[s]
-                quantise(codes, scales, grouped[s][:])
-
-            for s in range(own, len(strips)):
-                interleave(SCALAR, grouped[s][:], strips[s][1])
-            for s in range(own):
-                interleave(VECTOR, grouped[s][:], strips[s][1])
-                if s > 0:
-                    quantise_strip(s - 1)
-            for t in h_tiles[:1]:
-                quantise_h(t)
-            for s in range(own - 1, len(strips)):
-                quantise_strip(s)
-            for t in h_tiles[1:]:
-                quantise_h(t)
-
         x_raw, x_mx = {}, {}
 
         def load_x(tiles, g):
@@ -95,13 +73,32 @@ def tile_mix_lowrank_tm_none_kernel(tc, x, w4_words, w4_scales, down, up, out):
             rows = x[g * ROWS : (g + 1) * ROWS, tiles[0] * P : (tiles[-1] + 1) * P]
             nc.sync.dma_start(out=raw[:], in_=rows.rearrange("(p j) t -> p j t", j=PACK))
             for s, t in enumerate(tiles):
-                x_raw[t, g] = raw[:, :, s * P : (s + 1) * P]
+                x_raw[t, g] = raw, s * P
+
+        x_grouped = {}
+
+        def copy_x(tiles, g, engine):
+            raw, first = x_raw[tiles[0], g]
+            x_grouped[tiles, g] = sbuf(f"x{tiles[0]}{g}_grouped", [P, len(tiles) * P, PACK], BF16)
+            interleave(engine, x_grouped[tiles, g][:], raw[:, :, first : first + len(tiles) * P])
+
+        def quantise_x(tiles, g):
+            codes = sbuf(f"x{tiles[0]}{g}_codes", [P, len(tiles) * P], U32)
+            scales = sbuf(f"x{tiles[0]}{g}_scales", [P, len(tiles) * P], U8)
+            quantise(codes[:], scales[:], x_grouped[tiles, g][:])
+            for s, t in enumerate(tiles):
+                x_mx[t, g] = codes[:, s * P : (s + 1) * P], scales[:, s * P : (s + 1) * P]
 
         def prepare_x(tiles, g, scalar_strips=0):
-            for t in tiles:
-                x_mx[t, g] = sbuf(f"x{t}{g}_codes", [P, P], U32), sbuf(f"x{t}{g}_scales", [P, P], U8)
-            strips = [(f"x{t}{g}", x_raw[t, g], x_mx[t, g][0][:], x_mx[t, g][1][:]) for t in tiles]
-            prepare(strips, scalar_strips, ())
+            own = len(tiles) - scalar_strips
+            for t in tiles[own:]:
+                copy_x((t,), g, SCALAR)
+            for s, t in enumerate(tiles[:own]):
+                copy_x((t,), g, VECTOR)
+                if s > 0:
+                    quantise_x((tiles[s - 1],), g)
+            for t in tiles[own - 1 :]:
+                quantise_x((t,), g)
 
         down_raw = {}
         down_grouped = [sbuf(f"down{g}_grouped", [P, R, PACK], BF16) for g in PASSES]
@@ -123,56 +120,51 @@ def tile_mix_lowrank_tm_none_kernel(tc, x, w4_words, w4_scales, down, up, out):
                 columns = slice(first, first + P)
                 quantise(down_codes[g][:, columns], down_scales[g][:, columns], down_grouped[g][:, columns])
 
-        up_raw = {}
-        up_codes = [sbuf(f"up{n}_codes", [P, HALF], U32) for n in HALVES]
-        up_scales = [sbuf(f"up{n}_scales", [P, HALF], U8) for n in HALVES]
+        up_raw = [sbuf(f"up{n}_raw", [P, PACK, HALF], F32) for n in HALVES]
+        up_grouped = sbuf("up_grouped", [P, N, PACK], BF16)
+        up_codes = sbuf("up_codes", [P, N], U32)
+        up_scales = sbuf("up_scales", [P, N], U8)
 
         def load_up(n):
-            up_raw[n] = sbuf(f"up{n}_raw", [P, PACK, HALF], F32)
             rows = up[:, n * HALF : (n + 1) * HALF]
             nc.sync.dma_start(out=up_raw[n][:], in_=rows.rearrange("(p j) n -> p j n", j=PACK))
 
-        def prepare_up_alone(n, h_tiles):
-            columns = [slice(first, first + P) for first in range(0, HALF, P)]
-            strips = [(f"up{n}{c.start}", up_raw[n][:, :, c], up_codes[n][:, c], up_scales[n][:, c]) for c in columns]
-            prepare(strips, 0, h_tiles)
+        def copy_up(engine, first, last):
+            n, inside = divmod(first, HALF)
+            interleave(engine, up_grouped[:, first:last], up_raw[n][:, :, inside : inside + last - first])
 
-        def prepare_up_shared(n, h_tile):
-            grouped = sbuf(f"up{n}_grouped", [P, HALF, PACK], BF16)
-            middle, split = HALF // 2, HALF - UP_SCALAR_SHARE
-            interleave(SCALAR, grouped[:, split:], up_raw[n][:, :, split:])
-            interleave(VECTOR, grouped[:, :middle], up_raw[n][:, :, :middle])
-            interleave(VECTOR, grouped[:, middle:split], up_raw[n][:, :, middle:split])
-            quantise_h(h_tile)
-            for columns in (slice(0, middle), slice(middle, HALF)):
-                quantise(up_codes[n][:, columns], up_scales[n][:, columns], grouped[:, columns])
+        def quantise_up(first, last):
+            quantise(up_codes[:, first:last], up_scales[:, first:last], up_grouped[:, first:last])
 
-        w4_codes = sbuf("w4_codes", [P, len(PASSES), 2 * N], U8)
+        w4_codes = [sbuf(f"w4{g}_codes", [P, 2 * N], U8) for g in PASSES]
         w4_scale_rows = sbuf("w4_scale_rows", [P, len(PASSES), N], U8)
 
-        def load_w4():
-            for quadrant in range(4):
+        def load_w4_scales():
+            for s in range(4):
                 nc.sync.dma_start(
-                    out=w4_scale_rows[32 * quadrant : 32 * quadrant + 4].bitcast(I32),
-                    in_=w4_scales[:, 4 * quadrant : 4 * quadrant + 4, :].rearrange("g s n -> s g n").bitcast(I32),
+                    out=w4_scale_rows[s:P:32].bitcast(I32),
+                    in_=w4_scales[:, s:16:4, :].rearrange("g q n -> q g n").bitcast(I32),
                 )
-            nc.sync.dma_start(out=w4_codes[:].bitcast(I32), in_=w4_words.rearrange("g p n -> p g n").bitcast(I32))
 
-        h_sums, h_grouped, h_mx = {}, {}, {}
+        def load_w4(g):
+            nc.sync.dma_start(out=w4_codes[g][:].bitcast(I32), in_=w4_words[g].bitcast(I32))
 
-        def make_h(t, g):
-            if g == PASSES[0]:
+        h_sums, h_first_pass, h_grouped, h_mx = {}, {}, {}, {}
+
+        def make_h(t, g, outputs=range(PACK)):
+            if t not in h_sums:
                 h_sums[t] = take_bank(("h", t), f"h{t}_sums", [P, PACK, P])
+                h_first_pass[t] = g
             codes, scales = x_mx[t, g]
-            for i in range(PACK):
+            for i in outputs:
                 nc.tensor.matmul_mx(
                     out=h_sums[t][:, i, :],
                     lhsT=down_codes[g][:, i * P : (i + 1) * P].bitcast(E4M3),
                     lhsT_scale=down_scales[g][:, i * P : (i + 1) * P],
                     rhs=codes[:].bitcast(E4M3),
                     rhs_scale=scales[:],
-                    start=(g == PASSES[0] and i == 0),
-                    stop=(g == PASSES[-1] and i == PACK - 1),
+                    start=(g == h_first_pass[t] and i == 0),
+                    stop=(g != h_first_pass[t] and i == PACK - 1),
                 )
 
         def empty_h(t, engine):
@@ -189,39 +181,40 @@ def tile_mix_lowrank_tm_none_kernel(tc, x, w4_words, w4_scales, down, up, out):
 
         def base(t, n, passes=PASSES):
             for g in passes:
-                if g == PASSES[0]:
+                opens = (t, n) not in sums
+                if opens:
                     sums[t, n] = take_bank((t, n), f"sums{t}{n}", [P, HALF])
                 codes, scales = x_mx[t, g]
                 nc.tensor.matmul_mx(
                     out=sums[t, n][:],
                     lhsT=codes[:].bitcast(E4M3),
                     lhsT_scale=scales[:],
-                    rhs=w4_codes[:, g, 2 * HALF * n : 2 * HALF * (n + 1)].bitcast(E2M1),
+                    rhs=w4_codes[g][:, 2 * HALF * n : 2 * HALF * (n + 1)].bitcast(E2M1),
                     rhs_scale=w4_scale_rows[:, g, HALF * n : HALF * (n + 1)],
-                    start=(g == PASSES[0]),
+                    start=opens,
                     stop=False,
                 )
 
-        def branch(t, n):
+        def branch(t, n, inside=0, width=HALF):
             codes, scales = h_mx[t]
+            columns = slice(n * HALF + inside, n * HALF + inside + width)
             nc.tensor.matmul_mx(
-                out=sums[t, n][:],
+                out=sums[t, n][:, inside : inside + width],
                 lhsT=codes[:].bitcast(E4M3),
                 lhsT_scale=scales[:],
-                rhs=up_codes[n][:].bitcast(E4M3),
-                rhs_scale=up_scales[n][:],
+                rhs=up_codes[:, columns].bitcast(E4M3),
+                rhs_scale=up_scales[:, columns],
                 start=False,
-                stop=True,
+                stop=(inside + width == HALF),
             )
 
         def empty(t, n, engine):
             copy(engine, results[:, t, n * HALF : (n + 1) * HALF], sums[t, n][:])
             give_back((t, n))
 
-        def quarter(t, first, engine):
-            n, inside = divmod(first, HALF)
-            bank = take_bank((t, "quarter", first), f"quarter{first}", [P, QUARTER])
-            for strip in range(0, QUARTER, P):
+        def piece(t, first, width, engine):
+            bank = take_bank((t, "piece", first), f"piece{t}{first}", [P, width])
+            for strip in range(0, width, P):
                 column = first + strip
                 for g in PASSES:
                     codes, scales = x_mx[t, g]
@@ -229,7 +222,7 @@ def tile_mix_lowrank_tm_none_kernel(tc, x, w4_words, w4_scales, down, up, out):
                         out=bank[:, strip : strip + P],
                         lhsT=codes[:].bitcast(E4M3),
                         lhsT_scale=scales[:],
-                        rhs=w4_codes[:, g, 2 * column : 2 * (column + P)].bitcast(E2M1),
+                        rhs=w4_codes[g][:, 2 * column : 2 * (column + P)].bitcast(E2M1),
                         rhs_scale=w4_scale_rows[:, g, column : column + P],
                         start=(strip == 0 and g == PASSES[0]),
                         stop=False,
@@ -239,13 +232,14 @@ def tile_mix_lowrank_tm_none_kernel(tc, x, w4_words, w4_scales, down, up, out):
                 out=bank[:],
                 lhsT=codes[:].bitcast(E4M3),
                 lhsT_scale=scales[:],
-                rhs=up_codes[n][:, inside : inside + QUARTER].bitcast(E4M3),
-                rhs_scale=up_scales[n][:, inside : inside + QUARTER],
+                rhs=up_codes[:, first : first + width].bitcast(E4M3),
+                rhs_scale=up_scales[:, first : first + width],
                 start=False,
                 stop=True,
             )
-            copy(engine, results[:, t, first : first + QUARTER], bank[:])
-            store(t, first, QUARTER)
+            copy(engine, results[:, t, first : first + width], bank[:])
+            give_back((t, "piece", first))
+            store(t, first, width)
 
         def store(t, first, width):
             nc.sync.dma_start(
@@ -254,66 +248,105 @@ def tile_mix_lowrank_tm_none_kernel(tc, x, w4_words, w4_scales, down, up, out):
 
         nc.vector.memset(w4_scale_rows[:].rearrange("p g n -> p (g n)").bitcast(I32), 0)
 
+        a, b = SECOND
+        c, d = THIRD
         load_x(FIRST, 0)
-        load_w4()
-        load_x(FIRST, 1)
-        for g in PASSES:
-            load_down(g)
+        load_w4_scales()
+        load_w4(0)
+        load_down(0)
+        load_x(FIRST[:2], 1)
+        load_down(1)
+        load_w4(1)
+        load_x(FIRST[2:], 1)
         for n in HALVES:
             load_up(n)
         for tiles in (SECOND, THIRD):
             for g in PASSES:
                 load_x(tiles, g)
 
-
-        for g in PASSES:
-            prepare_x(FIRST, g, scalar_strips=1)
-            for t in FIRST:
-                base(t, 0, [g])
-        for g in PASSES:
-            prepare_down(g)
-            for t in FIRST:
-                make_h(t, g)
+        prepare_x(FIRST, 0, scalar_strips=1)
+        for t in FIRST[:2]:
+            base(t, 0, [0])
+        prepare_down(0)
         for t in FIRST:
-            empty_h(t, SCALAR)
-
-        leading, trailing = FIRST[:-1], FIRST[-1]
-        for t in leading:
+            make_h(t, 0)
+        for t in FIRST[2:]:
+            base(t, 0, [0])
+        prepare_x(FIRST[:2], 1, scalar_strips=1)
+        prepare_down(1)
+        copy_x((2,), 1, VECTOR)
+        copy_x((3,), 1, SCALAR)
+        quantise_x((2,), 1)
+        quantise_x((3,), 1)
+        for i in range(PACK):
+            for t in FIRST[:2]:
+                make_h(t, 1, [i])
+        for t in FIRST[:2]:
+            base(t, 0, [1])
+        for t in FIRST[2:]:
+            make_h(t, 1)
+            base(t, 0, [1])
+        empty_h(0, VECTOR)
+        empty_h(1, SCALAR)
+        empty_h(2, SCALAR)
+        copy_up(SCALAR, 384, 512)
+        empty_h(3, SCALAR)
+        for t in FIRST:
             base(t, 1)
-        prepare_up_alone(0, leading)
-        for t in leading:
-            branch(t, 0)
-        base(trailing, 1)
-        prepare_up_shared(1, trailing)
-        branch(trailing, 0)
-        for t in FIRST:
-            branch(t, 1)
 
-        a, b = SECOND
-        prepare_x(SECOND, 0)
+        copy_up(VECTOR, 0, 256)
+        copy_up(VECTOR, 256, 384)
+        quantise_up(0, 256)
+        quantise_h(0)
+        quantise_up(256, 512)
+        quantise_h(1)
+        quantise_h(2)
+        quantise_h(3)
+        for t in FIRST:
+            branch(t, 0)
+        copy_up(SCALAR, 832, 1024)
+        copy_up(VECTOR, 512, 768)
+        copy_up(VECTOR, 768, 832)
+        quantise_up(512, 768)
+        quantise_up(768, 1024)
+        for inside in (0, QUARTER):
+            for t in FIRST:
+                branch(t, 1, inside, QUARTER)
+
+        copy_x((a,), 0, VECTOR)
+        copy_x((b,), 0, VECTOR)
+        quantise_x((a,), 0)
+        copy_x((a,), 1, VECTOR)
+        quantise_x((b,), 0)
+        quantise_x((a,), 1)
+        copy_x((b,), 1, VECTOR)
         for n in HALVES:
-            for t in leading:
+            for t in FIRST[:3]:
                 empty(t, n, SCALAR)
-        for g in PASSES:
-            if g > 0:
-                prepare_x(SECOND, g)
-            for t in SECOND:
-                make_h(t, g)
-            for n in HALVES:
-                base(a, n, [g])
-        for n, t in enumerate(SECOND):
-            empty(trailing, n, SCALAR)
-            empty_h(t, SCALAR)
-        prepare_x(THIRD, 0)
+        make_h(a, 0)
+        base(a, 0, [0])
+        make_h(b, 0)
+        base(a, 1, [0])
+        make_h(a, 1)
+        for n in HALVES:
+            base(a, n, [1])
+        copy_x(THIRD, 0, VECTOR)
+        quantise_x((b,), 1)
+        make_h(b, 1)
+        empty_h(a, VECTOR)
+        empty(3, 0, SCALAR)
+        empty_h(b, SCALAR)
+        empty(3, 1, SCALAR)
+        quantise_x(THIRD, 0)
         quantise_h(a)
+        copy_x(THIRD, 1, VECTOR)
+        quantise_h(b)
+        quantise_x(THIRD, 1)
         for n in HALVES:
             base(b, n)
         for n in HALVES:
             branch(a, n)
 
-        c, d = THIRD
-        prepare_x(THIRD, 1)
-        quantise_h(b)
         empty(a, 0, SCALAR)
         empty(a, 1, VECTOR)
         for g in PASSES:
@@ -328,14 +361,15 @@ def tile_mix_lowrank_tm_none_kernel(tc, x, w4_words, w4_scales, down, up, out):
         empty(b, 1, SCALAR)
         empty_h(d, VECTOR)
         quantise_h(d)
-        for n in HALVES:
-            base(c, n)
-            branch(c, n)
-            empty(c, n, VECTOR if n else SCALAR)
+        base(c, 0)
+        branch(c, 0)
+        empty(c, 0, SCALAR)
 
         for t in FIRST + SECOND:
             store(t, 0, N)
-        for n in HALVES:
-            store(c, n * HALF, HALF)
-        for q, first in enumerate(range(0, N, QUARTER)):
-            quarter(d, first, VECTOR if q % 2 else SCALAR)
+        store(c, 0, HALF)
+        pieces = [(c, first, QUARTER) for first in range(HALF, N, QUARTER)]
+        pieces += [(d, first, QUARTER) for first in range(0, N - QUARTER, QUARTER)]
+        pieces += [(d, first, P) for first in range(N - QUARTER, N, P)]
+        for q, (t, first, width) in enumerate(pieces):
+            piece(t, first, width, SCALAR if q % 2 else VECTOR)

@@ -24,6 +24,7 @@ BANKS = 8
 
 FIRST, SECOND, THIRD = (0, 1, 2, 3), (4, 5), (6, 7)
 
+UP_FIRST = 640
 DOWN_SCALAR_SHARE = 44
 
 
@@ -120,17 +121,19 @@ def tile_mix_lowrank_tm_none_kernel(tc, x, w4_words, w4_scales, down, up, out):
                 columns = slice(first, first + P)
                 quantise(down_codes[g][:, columns], down_scales[g][:, columns], down_grouped[g][:, columns])
 
-        up_raw = [sbuf(f"up{n}_raw", [P, PACK, HALF], F32) for n in HALVES]
+        up_parts = (slice(0, UP_FIRST), slice(UP_FIRST, N))
+        up_raw = [sbuf(f"up{part.start}_raw", [P, PACK, part.stop - part.start], F32) for part in up_parts]
         up_grouped = sbuf("up_grouped", [P, N, PACK], BF16)
         up_codes = sbuf("up_codes", [P, N], U32)
         up_scales = sbuf("up_scales", [P, N], U8)
 
         def load_up(n):
-            rows = up[:, n * HALF : (n + 1) * HALF]
+            rows = up[:, up_parts[n]]
             nc.sync.dma_start(out=up_raw[n][:], in_=rows.rearrange("(p j) n -> p j n", j=PACK))
 
         def copy_up(engine, first, last):
-            n, inside = divmod(first, HALF)
+            n = int(first >= UP_FIRST)
+            inside = first - up_parts[n].start
             interleave(engine, up_grouped[:, first:last], up_raw[n][:, :, inside : inside + last - first])
 
         def quantise_up(first, last):
@@ -287,52 +290,51 @@ def tile_mix_lowrank_tm_none_kernel(tc, x, w4_words, w4_scales, down, up, out):
             make_h(t, 1)
             base(t, 0, [1])
         empty_h(0, VECTOR)
-        empty_h(1, SCALAR)
-        empty_h(2, SCALAR)
-        copy_up(SCALAR, 384, 512)
-        empty_h(3, SCALAR)
-        for t in FIRST:
+        for t in FIRST[1:]:
+            empty_h(t, SCALAR)
+        for t in FIRST[:3]:
             base(t, 1)
+        base(3, 1, [0])
+        for t in FIRST[:3]:
+            quantise_h(t)
 
+        copy_up(SCALAR, 384, 512)
+        copy_up(SCALAR, 512, 640)
         copy_up(VECTOR, 0, 256)
         copy_up(VECTOR, 256, 384)
         quantise_up(0, 256)
-        quantise_h(0)
-        quantise_up(256, 512)
-        quantise_h(1)
-        quantise_h(2)
         quantise_h(3)
-        for t in FIRST:
-            branch(t, 0)
-        copy_up(SCALAR, 832, 1024)
-        copy_up(VECTOR, 512, 768)
-        copy_up(VECTOR, 768, 832)
+        quantise_up(256, 512)
+        for inside in (0, QUARTER):
+            for t in FIRST[:3]:
+                branch(t, 0, inside, QUARTER)
+        base(3, 1, [1])
+        branch(3, 0)
+        copy_up(SCALAR, 896, 1024)
+        copy_up(VECTOR, 640, 768)
+        copy_up(VECTOR, 768, 896)
         quantise_up(512, 768)
         quantise_up(768, 1024)
         for inside in (0, QUARTER):
             for t in FIRST:
                 branch(t, 1, inside, QUARTER)
 
-        copy_x((a,), 0, VECTOR)
-        copy_x((b,), 0, VECTOR)
-        quantise_x((a,), 0)
-        copy_x((a,), 1, VECTOR)
-        quantise_x((b,), 0)
-        quantise_x((a,), 1)
-        copy_x((b,), 1, VECTOR)
-        for n in HALVES:
-            for t in FIRST[:3]:
-                empty(t, n, SCALAR)
+        prepare_x(SECOND, 0)
+        prepare_x(SECOND, 1)
+        for t in FIRST[:3]:
+            empty(t, 0, SCALAR)
+        for t in FIRST[:3]:
+            empty(t, 1, SCALAR)
         make_h(a, 0)
         base(a, 0, [0])
         make_h(b, 0)
         base(a, 1, [0])
+        base(b, 0, [0])
         make_h(a, 1)
+        make_h(b, 1)
         for n in HALVES:
             base(a, n, [1])
         copy_x(THIRD, 0, VECTOR)
-        quantise_x((b,), 1)
-        make_h(b, 1)
         empty_h(a, VECTOR)
         empty(3, 0, SCALAR)
         empty_h(b, SCALAR)
@@ -342,16 +344,15 @@ def tile_mix_lowrank_tm_none_kernel(tc, x, w4_words, w4_scales, down, up, out):
         copy_x(THIRD, 1, VECTOR)
         quantise_h(b)
         quantise_x(THIRD, 1)
-        for n in HALVES:
-            base(b, n)
+        base(b, 0, [1])
+        base(b, 1)
         for n in HALVES:
             branch(a, n)
 
         empty(a, 0, SCALAR)
         empty(a, 1, VECTOR)
-        for g in PASSES:
+        for g, n in zip(PASSES, HALVES):
             make_h(c, g)
-        for n in HALVES:
             branch(b, n)
         empty_h(c, SCALAR)
         empty(b, 0, VECTOR)

@@ -38,7 +38,7 @@ def tile_mix_lowrank_tm_none_kernel(tc, x, w4_words, w4_scales, down, up, out):
         ctx.enter_context(tc.manual_schedule())
 
         def sbuf(name, shape, dtype):
-            return keep.tile(shape, dtype, name=name, tag=name, align_bytes=64)
+            return keep.tile(shape, dtype, name=name, tag=name, align_bytes=256)
 
         free_banks = list(range(BANKS))
         bank_of = {}
@@ -104,7 +104,7 @@ def tile_mix_lowrank_tm_none_kernel(tc, x, w4_words, w4_scales, down, up, out):
         down_raw = {}
         down_grouped = [sbuf(f"down{g}_grouped", [P, R, PACK], BF16) for g in PASSES]
         down_codes = [sbuf(f"down{g}_codes", [P, R], U32) for g in PASSES]
-        down_scales = [sbuf(f"down{g}_scales", [P, R], U8) for g in PASSES]
+        down_scales = [[sbuf(f"down{g}{i}_scales", [P, P], U8) for i in range(PACK)] for g in PASSES]
 
         def load_down(g):
             down_raw[g] = sbuf(f"down{g}_raw", [P, PACK, R], F32)
@@ -117,9 +117,9 @@ def tile_mix_lowrank_tm_none_kernel(tc, x, w4_words, w4_scales, down, up, out):
             split = P - DOWN_SCALAR_SHARE
             copy(VECTOR, grouped[:, :split], raw[:, :split])
             copy(SCALAR, grouped[:, split:], raw[:, split:])
-            for first in range(0, R, P):
-                columns = slice(first, first + P)
-                quantise(down_codes[g][:, columns], down_scales[g][:, columns], down_grouped[g][:, columns])
+            for i in range(PACK):
+                columns = slice(i * P, (i + 1) * P)
+                quantise(down_codes[g][:, columns], down_scales[g][i][:], down_grouped[g][:, columns])
 
         up_parts = (slice(0, UP_FIRST), slice(UP_FIRST, N))
         up_raw = [sbuf(f"up{part.start}_raw", [P, PACK, part.stop - part.start], F32) for part in up_parts]
@@ -163,7 +163,7 @@ def tile_mix_lowrank_tm_none_kernel(tc, x, w4_words, w4_scales, down, up, out):
                 nc.tensor.matmul_mx(
                     out=h_sums[t][:, i, :],
                     lhsT=down_codes[g][:, i * P : (i + 1) * P].bitcast(E4M3),
-                    lhsT_scale=down_scales[g][:, i * P : (i + 1) * P],
+                    lhsT_scale=down_scales[g][i][:],
                     rhs=codes[:].bitcast(E4M3),
                     rhs_scale=scales[:],
                     start=(g == h_first_pass[t] and i == 0),
@@ -362,15 +362,16 @@ def tile_mix_lowrank_tm_none_kernel(tc, x, w4_words, w4_scales, down, up, out):
         empty(b, 1, SCALAR)
         empty_h(d, VECTOR)
         quantise_h(d)
-        base(c, 0)
-        branch(c, 0)
-        empty(c, 0, SCALAR)
+        for n in HALVES:
+            base(c, n)
+            branch(c, n)
+            empty(c, n, VECTOR if n else SCALAR)
 
         for t in FIRST + SECOND:
             store(t, 0, N)
-        store(c, 0, HALF)
-        pieces = [(c, first, QUARTER) for first in range(HALF, N, QUARTER)]
-        pieces += [(d, first, QUARTER) for first in range(0, N - QUARTER, QUARTER)]
-        pieces += [(d, first, P) for first in range(N - QUARTER, N, P)]
-        for q, (t, first, width) in enumerate(pieces):
-            piece(t, first, width, SCALAR if q % 2 else VECTOR)
+        for n in HALVES:
+            store(c, n * HALF, HALF)
+        first = 0
+        for q, width in enumerate((QUARTER, QUARTER, QUARTER, QUARTER)):
+            piece(d, first, width, VECTOR if q % 2 else SCALAR)
+            first = first + width

@@ -25,7 +25,7 @@ BANKS = 8
 FIRST, SECOND, THIRD = (0, 1, 2, 3), (4, 5), (6, 7)
 
 UP_FIRST = 640
-DOWN_SCALAR_SHARE = 44
+DOWN_SCALAR_SHARE = 96
 
 
 def tile_mix_lowrank_tm_none_kernel(tc, x, w4_words, w4_scales, down, up, out):
@@ -112,11 +112,12 @@ def tile_mix_lowrank_tm_none_kernel(tc, x, w4_words, w4_scales, down, up, out):
             nc.sync.dma_start(out=down_raw[g][:], in_=rows.rearrange("(p j) r -> p j r", j=PACK))
 
         def prepare_down(g):
-            grouped = down_grouped[g][:].rearrange("p (i m) j -> p m i j", i=PACK)
-            raw = down_raw[g][:].rearrange("p j (m i) -> p m i j", i=PACK)
+            grouped = down_grouped[g][:].rearrange("p (i m) j -> p m j i", i=PACK)
+            raw = down_raw[g][:].rearrange("p j (m i) -> p m j i", i=PACK)
             split = P - DOWN_SCALAR_SHARE
-            copy(VECTOR, grouped[:, :split], raw[:, :split])
-            copy(SCALAR, grouped[:, split:], raw[:, split:])
+            copy(SCALAR, grouped[:, split:, :, 2:], raw[:, split:, :, 2:])
+            copy(VECTOR, grouped[:, :, :, :2], raw[:, :, :, :2])
+            copy(VECTOR, grouped[:, :split, :, 2:], raw[:, :split, :, 2:])
             for i in range(PACK):
                 columns = slice(i * P, (i + 1) * P)
                 quantise(down_codes[g][:, columns], down_scales[g][i][:], down_grouped[g][:, columns])
@@ -334,16 +335,19 @@ def tile_mix_lowrank_tm_none_kernel(tc, x, w4_words, w4_scales, down, up, out):
         make_h(b, 1)
         for n in HALVES:
             base(a, n, [1])
-        copy_x(THIRD, 0, VECTOR)
+        for t in THIRD:
+            copy_x((t,), 0, VECTOR)
+        quantise_x((c,), 0)
         empty_h(a, VECTOR)
         empty(3, 0, SCALAR)
         empty_h(b, SCALAR)
         empty(3, 1, SCALAR)
-        quantise_x(THIRD, 0)
+        quantise_x((d,), 0)
         quantise_h(a)
-        copy_x(THIRD, 1, VECTOR)
+        copy_x((c,), 1, VECTOR)
         quantise_h(b)
-        quantise_x(THIRD, 1)
+        quantise_x((c,), 1)
+        copy_x((d,), 1, VECTOR)
         base(b, 0, [1])
         base(b, 1)
         for n in HALVES:
@@ -351,8 +355,10 @@ def tile_mix_lowrank_tm_none_kernel(tc, x, w4_words, w4_scales, down, up, out):
 
         empty(a, 0, SCALAR)
         empty(a, 1, VECTOR)
-        for g, n in zip(PASSES, HALVES):
+        quantise_x((d,), 1)
+        for g in PASSES:
             make_h(c, g)
+        for n in HALVES:
             branch(b, n)
         empty_h(c, SCALAR)
         empty(b, 0, VECTOR)

@@ -24,7 +24,7 @@ BANKS = 8
 
 FIRST, SECOND, THIRD = (0, 1, 2, 3), (4, 5), (6, 7)
 
-UP_FIRST = 640
+UP_FIRST = 512
 DOWN_SCALAR_SHARE = 96
 
 
@@ -111,14 +111,16 @@ def tile_mix_lowrank_tm_none_kernel(tc, x, w4_words, w4_scales, down, up, out):
             rows = down[g * ROWS : (g + 1) * ROWS, :]
             nc.sync.dma_start(out=down_raw[g][:], in_=rows.rearrange("(p j) r -> p j r", j=PACK))
 
-        def prepare_down(g):
+        def copy_down(g):
             grouped = down_grouped[g][:].rearrange("p (i m) j -> p m j i", i=PACK)
             raw = down_raw[g][:].rearrange("p j (m i) -> p m j i", i=PACK)
             split = P - DOWN_SCALAR_SHARE
             copy(SCALAR, grouped[:, split:, :, 2:], raw[:, split:, :, 2:])
             copy(VECTOR, grouped[:, :, :, :2], raw[:, :, :, :2])
             copy(VECTOR, grouped[:, :split, :, 2:], raw[:, :split, :, 2:])
-            for i in range(PACK):
+
+        def quantise_down(g, operands=range(PACK)):
+            for i in operands:
                 columns = slice(i * P, (i + 1) * P)
                 quantise(down_codes[g][:, columns], down_scales[g][i][:], down_grouped[g][:, columns])
 
@@ -140,7 +142,8 @@ def tile_mix_lowrank_tm_none_kernel(tc, x, w4_words, w4_scales, down, up, out):
         def quantise_up(first, last):
             quantise(up_codes[:, first:last], up_scales[:, first:last], up_grouped[:, first:last])
 
-        w4_codes = [sbuf(f"w4{g}_codes", [P, 2 * N], U8) for g in PASSES]
+        w4_all = sbuf("w4_codes", [P, len(PASSES), 2 * N], U8)
+        w4_codes = [w4_all[:, g, :] for g in PASSES]
         w4_scale_rows = sbuf("w4_scale_rows", [P, len(PASSES), N], U8)
 
         def load_w4_scales():
@@ -150,8 +153,8 @@ def tile_mix_lowrank_tm_none_kernel(tc, x, w4_words, w4_scales, down, up, out):
                     in_=w4_scales[:, s:16:4, :].rearrange("g q n -> q g n").bitcast(I32),
                 )
 
-        def load_w4(g):
-            nc.sync.dma_start(out=w4_codes[g][:].bitcast(I32), in_=w4_words[g].bitcast(I32))
+        def load_w4():
+            nc.sync.dma_start(out=w4_all[:].bitcast(I32), in_=w4_words.rearrange("g p b -> p g b").bitcast(I32))
 
         h_sums, h_first_pass, h_grouped, h_mx = {}, {}, {}, {}
 
@@ -243,141 +246,167 @@ def tile_mix_lowrank_tm_none_kernel(tc, x, w4_words, w4_scales, down, up, out):
             )
             copy(engine, results[:, t, first : first + width], bank[:])
             give_back((t, "piece", first))
-            store(t, first, width)
 
-        def store(t, first, width):
+        def store(tiles, first, width):
+            rows = out[tiles[0] * P : (tiles[-1] + 1) * P, first : first + width]
             nc.sync.dma_start(
-                out=out[t * P : (t + 1) * P, first : first + width], in_=results[:, t, first : first + width]
+                out=rows.rearrange("(t p) n -> p t n", p=P),
+                in_=results[:, tiles[0] : tiles[-1] + 1, first : first + width],
             )
 
         nc.vector.memset(w4_scale_rows[:].rearrange("p g n -> p (g n)").bitcast(I32), 0)
 
         a, b = SECOND
         c, d = THIRD
-        load_x(FIRST, 0)
-        load_w4_scales()
-        load_w4(0)
         load_down(0)
-        load_x(FIRST[:2], 1)
+        load_x(FIRST, 0)
         load_down(1)
-        load_w4(1)
+        load_x(FIRST[:2], 1)
+        load_w4_scales()
+        load_w4()
         load_x(FIRST[2:], 1)
-        for n in HALVES:
-            load_up(n)
-        for tiles in (SECOND, THIRD):
-            for g in PASSES:
-                load_x(tiles, g)
+        load_up(0)
+        for g in PASSES:
+            load_x(SECOND, g)
+        load_up(1)
+        for g in PASSES:
+            load_x(THIRD, g)
 
-        prepare_x(FIRST, 0, scalar_strips=1)
-        for t in FIRST[:2]:
-            base(t, 0, [0])
-        prepare_down(0)
+        copy_down(0)
+        quantise_down(0)
+        copy_x((3,), 0, SCALAR)
+        for t in FIRST[:3]:
+            copy_x((t,), 0, VECTOR)
+        for t in FIRST[:3]:
+            quantise_x((t,), 0)
+        copy_down(1)
+        quantise_x((3,), 0)
         for t in FIRST:
             make_h(t, 0)
-        for t in FIRST[2:]:
-            base(t, 0, [0])
-        prepare_x(FIRST[:2], 1, scalar_strips=1)
-        prepare_down(1)
-        copy_x((2,), 1, VECTOR)
-        copy_x((3,), 1, SCALAR)
-        quantise_x((2,), 1)
-        quantise_x((3,), 1)
-        for i in range(PACK):
-            for t in FIRST[:2]:
-                make_h(t, 1, [i])
+        quantise_down(1, [0, 1])
+        copy_x((1,), 1, SCALAR)
+        copy_x((0,), 1, VECTOR)
+        quantise_down(1, [2, 3])
         for t in FIRST[:2]:
-            base(t, 0, [1])
+            quantise_x((t,), 1)
+            make_h(t, 1)
+        empty_h(0, SCALAR)
+        empty_h(1, VECTOR)
+        for t in FIRST[:2]:
+            for n in HALVES:
+                base(t, n)
+        copy_x((3,), 1, SCALAR)
+        copy_x((2,), 1, VECTOR)
+        quantise_h(0)
+        quantise_x((2,), 1)
+        quantise_h(1)
+        quantise_x((3,), 1)
         for t in FIRST[2:]:
             make_h(t, 1)
-            base(t, 0, [1])
-        empty_h(0, VECTOR)
-        for t in FIRST[1:]:
-            empty_h(t, SCALAR)
-        for t in FIRST[:3]:
-            base(t, 1)
-        base(3, 1, [0])
-        for t in FIRST[:3]:
-            quantise_h(t)
+        empty_h(2, VECTOR)
+        empty_h(3, SCALAR)
+        for t in FIRST[2:]:
+            base(t, 0)
+        base(2, 1)
 
-        copy_up(SCALAR, 384, 512)
-        copy_up(SCALAR, 512, 640)
         copy_up(VECTOR, 0, 256)
+        copy_up(SCALAR, 384, 512)
         copy_up(VECTOR, 256, 384)
         quantise_up(0, 256)
-        quantise_h(3)
         quantise_up(256, 512)
+        quantise_h(2)
+        quantise_h(3)
+        base(3, 1, [0])
         for inside in (0, QUARTER):
-            for t in FIRST[:3]:
+            for t in FIRST[:2]:
                 branch(t, 0, inside, QUARTER)
+        for t in FIRST[2:]:
+            branch(t, 0)
         base(3, 1, [1])
-        branch(3, 0)
-        copy_up(SCALAR, 896, 1024)
-        copy_up(VECTOR, 640, 768)
-        copy_up(VECTOR, 768, 896)
-        quantise_up(512, 768)
-        quantise_up(768, 1024)
-        for inside in (0, QUARTER):
-            for t in FIRST:
-                branch(t, 1, inside, QUARTER)
-
-        prepare_x(SECOND, 0)
-        prepare_x(SECOND, 1)
-        for t in FIRST[:3]:
-            empty(t, 0, SCALAR)
-        for t in FIRST[:3]:
-            empty(t, 1, SCALAR)
+        copy_x((a,), 0, SCALAR)
+        quantise_x((a,), 0)
+        copy_x((a,), 1, VECTOR)
+        empty(0, 0, SCALAR)
+        empty(1, 0, VECTOR)
+        empty(2, 0, SCALAR)
+        empty(3, 0, SCALAR)
+        quantise_x((a,), 1)
+        for g in PASSES:
+            copy_x((b,), g, VECTOR)
+        for g in PASSES:
+            quantise_x((b,), g)
         make_h(a, 0)
         base(a, 0, [0])
-        make_h(b, 0)
-        base(a, 1, [0])
-        base(b, 0, [0])
         make_h(a, 1)
-        make_h(b, 1)
-        for n in HALVES:
-            base(a, n, [1])
-        for t in THIRD:
-            copy_x((t,), 0, VECTOR)
-        quantise_x((c,), 0)
-        empty_h(a, VECTOR)
-        empty(3, 0, SCALAR)
+        base(a, 0, [1])
+        base(a, 1, [0])
+        for g in PASSES:
+            make_h(b, g)
+        base(a, 1, [1])
+        empty_h(a, SCALAR)
+        base(b, 0)
+        copy_up(SCALAR, 896, 1024)
+        copy_up(VECTOR, 512, 768)
+        copy_up(VECTOR, 768, 896)
         empty_h(b, SCALAR)
-        empty(3, 1, SCALAR)
-        quantise_x((d,), 0)
+        quantise_up(512, 768)
+        quantise_up(768, 1024)
         quantise_h(a)
-        copy_x((c,), 1, VECTOR)
+        for inside in (0, QUARTER):
+            for t in FIRST[:2]:
+                branch(t, 1, inside, QUARTER)
+        for t in FIRST[2:]:
+            branch(t, 1)
+        copy_x((c,), 0, SCALAR)
         quantise_h(b)
-        quantise_x((c,), 1)
+        copy_x((d,), 0, VECTOR)
+        empty(0, 1, SCALAR)
+        empty(1, 1, VECTOR)
+        quantise_x((c,), 0)
+        copy_x((c,), 1, VECTOR)
+        quantise_x((d,), 0)
         copy_x((d,), 1, VECTOR)
-        base(b, 0, [1])
-        base(b, 1)
+        for t in THIRD:
+            quantise_x((t,), 1)
         for n in HALVES:
             branch(a, n)
-
-        empty(a, 0, SCALAR)
-        empty(a, 1, VECTOR)
-        quantise_x((d,), 1)
+        base(b, 1)
         for g in PASSES:
             make_h(c, g)
-        for n in HALVES:
-            branch(b, n)
-        empty_h(c, SCALAR)
-        empty(b, 0, VECTOR)
+            branch(b, g)
+        empty(2, 1, SCALAR)
+        empty(3, 1, SCALAR)
+        empty(a, 0, SCALAR)
+        empty(a, 1, VECTOR)
         for g in PASSES:
             make_h(d, g)
-        quantise_h(c)
+        empty_h(c, VECTOR)
+        empty(b, 0, SCALAR)
         empty(b, 1, SCALAR)
+        quantise_h(c)
         empty_h(d, VECTOR)
         quantise_h(d)
-        for n in HALVES:
-            base(c, n)
-            branch(c, n)
-            empty(c, n, VECTOR if n else SCALAR)
+        base(c, 0)
+        base(c, 1, [0])
+        branch(c, 0)
+        empty(c, 0, SCALAR)
+        base(c, 1, [1])
+        branch(c, 1)
+        empty(c, 1, VECTOR)
 
-        for t in FIRST + SECOND:
-            store(t, 0, N)
+        store(FIRST, 0, HALF)
+        store(FIRST[:2], HALF, HALF)
+        store(FIRST[2:], HALF, HALF)
+        for t in SECOND:
+            store((t,), 0, N)
         for n in HALVES:
-            store(c, n * HALF, HALF)
-        first = 0
-        for q, width in enumerate((QUARTER, QUARTER, QUARTER, QUARTER)):
-            piece(d, first, width, VECTOR if q % 2 else SCALAR)
-            first = first + width
+            store((c,), n * HALF, HALF)
+        base(d, 0)
+        branch(d, 0)
+        empty(d, 0, SCALAR)
+        store((d,), 0, HALF)
+        piece(d, 512, QUARTER, VECTOR)
+        store((d,), 512, QUARTER)
+        piece(d, 768, P, SCALAR)
+        piece(d, 896, P, VECTOR)
+        store((d,), 768, QUARTER)

@@ -142,8 +142,7 @@ def tile_mix_lowrank_tm_none_kernel(tc, x, w4_words, w4_scales, down, up, out):
         def quantise_up(first, last):
             quantise(up_codes[:, first:last], up_scales[:, first:last], up_grouped[:, first:last])
 
-        w4_all = sbuf("w4_codes", [P, len(PASSES), 2 * N], U8)
-        w4_codes = [w4_all[:, g, :] for g in PASSES]
+        w4_codes = [sbuf(f"w4{g}_codes", [P, 2 * N], U8) for g in PASSES]
         w4_scale_rows = sbuf("w4_scale_rows", [P, len(PASSES), N], U8)
 
         def load_w4_scales():
@@ -153,8 +152,8 @@ def tile_mix_lowrank_tm_none_kernel(tc, x, w4_words, w4_scales, down, up, out):
                     in_=w4_scales[:, s:16:4, :].rearrange("g q n -> q g n").bitcast(I32),
                 )
 
-        def load_w4():
-            nc.sync.dma_start(out=w4_all[:].bitcast(I32), in_=w4_words.rearrange("g p b -> p g b").bitcast(I32))
+        def load_w4(g):
+            nc.sync.dma_start(out=w4_codes[g][:].bitcast(I32), in_=w4_words[g].bitcast(I32))
 
         h_sums, h_first_pass, h_grouped, h_mx = {}, {}, {}, {}
 
@@ -258,13 +257,14 @@ def tile_mix_lowrank_tm_none_kernel(tc, x, w4_words, w4_scales, down, up, out):
 
         a, b = SECOND
         c, d = THIRD
-        load_down(0)
         load_x(FIRST, 0)
-        load_down(1)
-        load_x(FIRST[:2], 1)
         load_w4_scales()
-        load_w4()
+        load_w4(0)
+        load_down(0)
+        load_x(FIRST[:2], 1)
+        load_down(1)
         load_x(FIRST[2:], 1)
+        load_w4(1)
         load_up(0)
         for g in PASSES:
             load_x(SECOND, g)
@@ -272,42 +272,38 @@ def tile_mix_lowrank_tm_none_kernel(tc, x, w4_words, w4_scales, down, up, out):
         for g in PASSES:
             load_x(THIRD, g)
 
+        prepare_x(FIRST, 0, scalar_strips=1)
+        for t in FIRST[:2]:
+            base(t, 0, [0])
         copy_down(0)
         quantise_down(0)
-        copy_x((3,), 0, SCALAR)
-        for t in FIRST[:3]:
-            copy_x((t,), 0, VECTOR)
-        for t in FIRST[:3]:
-            quantise_x((t,), 0)
-        copy_down(1)
-        quantise_x((3,), 0)
         for t in FIRST:
             make_h(t, 0)
-        quantise_down(1, [0, 1])
-        copy_x((1,), 1, SCALAR)
-        copy_x((0,), 1, VECTOR)
-        quantise_down(1, [2, 3])
-        for t in FIRST[:2]:
-            quantise_x((t,), 1)
-            make_h(t, 1)
-        empty_h(0, SCALAR)
-        empty_h(1, VECTOR)
-        for t in FIRST[:2]:
-            for n in HALVES:
-                base(t, n)
-        copy_x((3,), 1, SCALAR)
-        copy_x((2,), 1, VECTOR)
-        quantise_h(0)
+        for t in FIRST[2:]:
+            base(t, 0, [0])
+        prepare_x(FIRST[:2], 1, scalar_strips=1)
+        copy_down(1)
+        quantise_down(1)
+        copy_x((2,), 1, SCALAR)
+        copy_x((3,), 1, VECTOR)
         quantise_x((2,), 1)
-        quantise_h(1)
         quantise_x((3,), 1)
+        for i in range(PACK):
+            for t in FIRST[:2]:
+                make_h(t, 1, [i])
+        for t in FIRST[:2]:
+            base(t, 0, [1])
         for t in FIRST[2:]:
             make_h(t, 1)
-        empty_h(2, VECTOR)
-        empty_h(3, SCALAR)
-        for t in FIRST[2:]:
-            base(t, 0)
-        base(2, 1)
+            base(t, 0, [1])
+        empty_h(0, VECTOR)
+        for t in FIRST[1:]:
+            empty_h(t, SCALAR)
+        for t in FIRST[:3]:
+            base(t, 1)
+        base(3, 1, [0])
+        for t in FIRST[:2]:
+            quantise_h(t)
 
         copy_up(VECTOR, 0, 256)
         copy_up(SCALAR, 384, 512)
@@ -316,7 +312,6 @@ def tile_mix_lowrank_tm_none_kernel(tc, x, w4_words, w4_scales, down, up, out):
         quantise_up(256, 512)
         quantise_h(2)
         quantise_h(3)
-        base(3, 1, [0])
         for inside in (0, QUARTER):
             for t in FIRST[:2]:
                 branch(t, 0, inside, QUARTER)

@@ -261,8 +261,8 @@ def tile_mix_lowrank_tm_none_kernel(tc, x, w4_words, w4_scales, down, up, out):
         load_w4_scales()
         load_w4(0)
         load_down(0)
-        load_x(FIRST[:2], 1)
         load_down(1)
+        load_x(FIRST[:2], 1)
         load_x(FIRST[2:], 1)
         load_w4(1)
         load_up(0)
@@ -281,33 +281,36 @@ def tile_mix_lowrank_tm_none_kernel(tc, x, w4_words, w4_scales, down, up, out):
             make_h(t, 0)
         for t in FIRST[2:]:
             base(t, 0, [0])
-        prepare_x(FIRST[:2], 1, scalar_strips=1)
         copy_down(1)
-        quantise_down(1)
-        copy_x((2,), 1, SCALAR)
-        copy_x((3,), 1, VECTOR)
+        quantise_down(1, [0, 1])
+        copy_x((1,), 1, SCALAR)
+        copy_x((0,), 1, VECTOR)
+        quantise_down(1, [2, 3])
+        quantise_x((0,), 1)
+        quantise_x((1,), 1)
+        copy_x((3,), 1, SCALAR)
+        copy_x((2,), 1, VECTOR)
         quantise_x((2,), 1)
         quantise_x((3,), 1)
-        for i in range(PACK):
-            for t in FIRST[:2]:
-                make_h(t, 1, [i])
+        for t in FIRST[:2]:
+            make_h(t, 1)
         for t in FIRST[:2]:
             base(t, 0, [1])
         for t in FIRST[2:]:
             make_h(t, 1)
             base(t, 0, [1])
-        empty_h(0, VECTOR)
-        for t in FIRST[1:]:
-            empty_h(t, SCALAR)
+        empty_h(0, SCALAR)
+        empty_h(1, VECTOR)
+        empty_h(2, SCALAR)
         for t in FIRST[:3]:
             base(t, 1)
-        base(3, 1, [0])
         for t in FIRST[:2]:
             quantise_h(t)
 
         copy_up(VECTOR, 0, 256)
         copy_up(SCALAR, 384, 512)
         copy_up(VECTOR, 256, 384)
+        empty_h(3, SCALAR)
         quantise_up(0, 256)
         quantise_up(256, 512)
         quantise_h(2)
@@ -315,69 +318,60 @@ def tile_mix_lowrank_tm_none_kernel(tc, x, w4_words, w4_scales, down, up, out):
         for inside in (0, QUARTER):
             for t in FIRST[:2]:
                 branch(t, 0, inside, QUARTER)
-        for t in FIRST[2:]:
-            branch(t, 0)
-        base(3, 1, [1])
+        for g in PASSES:
+            base(3, 1, [g])
+            branch(2 + g, 0)
         copy_x((a,), 0, SCALAR)
-        quantise_x((a,), 0)
+        copy_x((b,), 0, VECTOR)
         copy_x((a,), 1, VECTOR)
-        empty(0, 0, SCALAR)
-        empty(1, 0, VECTOR)
-        empty(2, 0, SCALAR)
-        empty(3, 0, SCALAR)
+        quantise_x((a,), 0)
+        copy_x((b,), 1, VECTOR)
         quantise_x((a,), 1)
-        for g in PASSES:
-            copy_x((b,), g, VECTOR)
-        for g in PASSES:
-            quantise_x((b,), g)
-        make_h(a, 0)
-        base(a, 0, [0])
-        make_h(a, 1)
-        base(a, 0, [1])
-        base(a, 1, [0])
-        for g in PASSES:
-            make_h(b, g)
-        base(a, 1, [1])
-        empty_h(a, SCALAR)
-        base(b, 0)
+        quantise_x((b,), 0)
+        quantise_x((b,), 1)
+        empty(0, 0, SCALAR)
+        empty(1, 0, SCALAR)
+        empty(2, 0, VECTOR)
+        empty(3, 0, SCALAR)
+        for t in SECOND:
+            for g in PASSES:
+                make_h(t, g)
+            base(t, 0)
         copy_up(SCALAR, 896, 1024)
         copy_up(VECTOR, 512, 768)
         copy_up(VECTOR, 768, 896)
-        empty_h(b, SCALAR)
+        for t in SECOND:
+            empty_h(t, SCALAR)
         quantise_up(512, 768)
         quantise_up(768, 1024)
         quantise_h(a)
-        for inside in (0, QUARTER):
-            for t in FIRST[:2]:
-                branch(t, 1, inside, QUARTER)
-        for t in FIRST[2:]:
+        base(a, 1)
+        for t in FIRST:
             branch(t, 1)
-        copy_x((c,), 0, SCALAR)
-        quantise_h(b)
-        copy_x((d,), 0, VECTOR)
-        empty(0, 1, SCALAR)
-        empty(1, 1, VECTOR)
-        quantise_x((c,), 0)
-        copy_x((c,), 1, VECTOR)
-        quantise_x((d,), 0)
-        copy_x((d,), 1, VECTOR)
-        for t in THIRD:
-            quantise_x((t,), 1)
         for n in HALVES:
             branch(a, n)
+        for t in THIRD:
+            copy_x((t,), 0, VECTOR)
+        quantise_h(b)
+        for t in THIRD:
+            copy_x((t,), 1, VECTOR)
+        for t in THIRD:
+            for g in PASSES:
+                quantise_x((t,), g)
+        for t in FIRST:
+            empty(t, 1, SCALAR)
+        for n in HALVES:
+            empty(a, n, VECTOR)
         base(b, 1)
         for g in PASSES:
             make_h(c, g)
-            branch(b, g)
-        empty(2, 1, SCALAR)
-        empty(3, 1, SCALAR)
-        empty(a, 0, SCALAR)
-        empty(a, 1, VECTOR)
+        for n in HALVES:
+            branch(b, n)
         for g in PASSES:
             make_h(d, g)
         empty_h(c, VECTOR)
-        empty(b, 0, SCALAR)
-        empty(b, 1, SCALAR)
+        for n in HALVES:
+            empty(b, n, SCALAR)
         quantise_h(c)
         empty_h(d, VECTOR)
         quantise_h(d)
@@ -390,8 +384,8 @@ def tile_mix_lowrank_tm_none_kernel(tc, x, w4_words, w4_scales, down, up, out):
         empty(c, 1, VECTOR)
 
         store(FIRST, 0, HALF)
-        store(FIRST[:2], HALF, HALF)
-        store(FIRST[2:], HALF, HALF)
+        for t in FIRST:
+            store((t,), HALF, HALF)
         for t in SECOND:
             store((t,), 0, N)
         for n in HALVES:

from contextlib import ExitStack

import concourse.mybir as mybir

K, R, N, T = 1024, 512, 1024, 1024
FLOPS = 2 * (K * R * T + K * N * T + R * N * T)

F32 = mybir.dt.float32
BF16 = mybir.dt.bfloat16
I32 = mybir.dt.int32
U32 = mybir.dt.uint32
U8 = mybir.dt.uint8
E4M3 = mybir.dt.float8_e4m3fn_x4
E2M1 = mybir.dt.float4_e2m1fn_x4

P = 128
PACK = 4
ROWS = P * PACK
PASSES = range(K // ROWS)
HALF = 512
HALVES = range(N // HALF)
QUARTER = 256
BANKS = 8

FIRST, SECOND, THIRD = (0, 1, 2, 3), (4, 5), (6, 7)

UP_FIRST = 512
DOWN_SCALAR_SHARE = 96


def tile_mix_lowrank_tm_none_kernel(tc, x, w4_words, w4_scales, down, up, out):
    nc = tc.nc
    SCALAR, VECTOR = "scalar", "vector"

    with ExitStack() as ctx:
        keep = ctx.enter_context(tc.tile_pool(name="keep", bufs=1))
        psum = ctx.enter_context(tc.psum_pool(name="psum", bufs=1))
        ctx.enter_context(tc.manual_schedule())

        def sbuf(name, shape, dtype):
            return keep.tile(shape, dtype, name=name, tag=name, align_bytes=256)

        free_banks = list(range(BANKS))
        bank_of = {}

        def take_bank(key, name, shape):
            bank_of[key] = free_banks[0]
            free_banks.remove(bank_of[key])
            return psum.tile(shape, F32, name=name, tag=f"bank{bank_of[key]}")

        def give_back(key):
            free_banks.append(bank_of[key])

        def copy(engine, dst, src):
            if engine == SCALAR:
                nc.scalar.copy(out=dst, in_=src)
            else:
                nc.vector.tensor_copy(out=dst, in_=src)

        def interleave(engine, grouped, raw):
            copy(
                engine,
                grouped.rearrange("p (c i) j -> p c j i", i=4),
                raw.rearrange("p j (c i) -> p c j i", i=4),
            )

        def quantise(codes, scales, grouped):
            nc.vector.quantize_mx(out=codes.bitcast(E4M3), scales=scales, in_=grouped.rearrange("p c j -> p (c j)"))

        x_raw, x_mx = {}, {}

        def load_x(tiles, g):
            raw = sbuf(f"x{tiles[0]}{g}_raw", [P, PACK, len(tiles) * P], F32)
            rows = x[g * ROWS : (g + 1) * ROWS, tiles[0] * P : (tiles[-1] + 1) * P]
            nc.sync.dma_start(out=raw[:], in_=rows.rearrange("(p j) t -> p j t", j=PACK))
            for s, t in enumerate(tiles):
                x_raw[t, g] = raw, s * P

        x_grouped = {}

        def copy_x(tiles, g, engine):
            raw, first = x_raw[tiles[0], g]
            x_grouped[tiles, g] = sbuf(f"x{tiles[0]}{g}_grouped", [P, len(tiles) * P, PACK], BF16)
            interleave(engine, x_grouped[tiles, g][:], raw[:, :, first : first + len(tiles) * P])

        def quantise_x(tiles, g):
            codes = sbuf(f"x{tiles[0]}{g}_codes", [P, len(tiles) * P], U32)
            scales = sbuf(f"x{tiles[0]}{g}_scales", [P, len(tiles) * P], U8)
            quantise(codes[:], scales[:], x_grouped[tiles, g][:])
            for s, t in enumerate(tiles):
                x_mx[t, g] = codes[:, s * P : (s + 1) * P], scales[:, s * P : (s + 1) * P]

        def prepare_x(tiles, g, scalar_strips=0):
            own = len(tiles) - scalar_strips
            for t in tiles[own:]:
                copy_x((t,), g, SCALAR)
            for s, t in enumerate(tiles[:own]):
                copy_x((t,), g, VECTOR)
                if s > 0:
                    quantise_x((tiles[s - 1],), g)
            for t in tiles[own - 1 :]:
                quantise_x((t,), g)

        down_raw = {}
        down_grouped = [sbuf(f"down{g}_grouped", [P, R, PACK], BF16) for g in PASSES]
        down_codes = [sbuf(f"down{g}_codes", [P, R], U32) for g in PASSES]
        down_scales = [[sbuf(f"down{g}{i}_scales", [P, P], U8) for i in range(PACK)] for g in PASSES]

        def load_down(g):
            down_raw[g] = sbuf(f"down{g}_raw", [P, PACK, R], F32)
            rows = down[g * ROWS : (g + 1) * ROWS, :]
            nc.sync.dma_start(out=down_raw[g][:], in_=rows.rearrange("(p j) r -> p j r", j=PACK))

        def copy_down(g):
            grouped = down_grouped[g][:].rearrange("p (i m) j -> p m j i", i=PACK)
            raw = down_raw[g][:].rearrange("p j (m i) -> p m j i", i=PACK)
            split = P - DOWN_SCALAR_SHARE
            copy(SCALAR, grouped[:, split:, :, 2:], raw[:, split:, :, 2:])
            copy(VECTOR, grouped[:, :, :, :2], raw[:, :, :, :2])
            copy(VECTOR, grouped[:, :split, :, 2:], raw[:, :split, :, 2:])

        def quantise_down(g, operands=range(PACK)):
            for i in operands:
                columns = slice(i * P, (i + 1) * P)
                quantise(down_codes[g][:, columns], down_scales[g][i][:], down_grouped[g][:, columns])

        up_parts = (slice(0, UP_FIRST), slice(UP_FIRST, N))
        up_raw = [sbuf(f"up{part.start}_raw", [P, PACK, part.stop - part.start], F32) for part in up_parts]
        up_grouped = sbuf("up_grouped", [P, N, PACK], BF16)
        up_codes = sbuf("up_codes", [P, N], U32)
        up_scales = sbuf("up_scales", [P, N], U8)

        def load_up(n):
            rows = up[:, up_parts[n]]
            nc.sync.dma_start(out=up_raw[n][:], in_=rows.rearrange("(p j) n -> p j n", j=PACK))

        def copy_up(engine, first, last):
            n = int(first >= UP_FIRST)
            inside = first - up_parts[n].start
            interleave(engine, up_grouped[:, first:last], up_raw[n][:, :, inside : inside + last - first])

        def quantise_up(first, last):
            quantise(up_codes[:, first:last], up_scales[:, first:last], up_grouped[:, first:last])

        w4_codes = [sbuf(f"w4{g}_codes", [P, 2 * N], U8) for g in PASSES]
        w4_scale_rows = sbuf("w4_scale_rows", [P, len(PASSES), N], U8)

        def load_w4_scales():
            for s in range(4):
                nc.sync.dma_start(
                    out=w4_scale_rows[s:P:32].bitcast(I32),
                    in_=w4_scales[:, s:16:4, :].rearrange("g q n -> q g n").bitcast(I32),
                )

        def load_w4(g):
            nc.sync.dma_start(out=w4_codes[g][:].bitcast(I32), in_=w4_words[g].bitcast(I32))

        h_sums, h_first_pass, h_grouped, h_mx = {}, {}, {}, {}

        def make_h(t, g, outputs=range(PACK)):
            if t not in h_sums:
                h_sums[t] = take_bank(("h", t), f"h{t}_sums", [P, PACK, P])
                h_first_pass[t] = g
            codes, scales = x_mx[t, g]
            for i in outputs:
                nc.tensor.matmul_mx(
                    out=h_sums[t][:, i, :],
                    lhsT=down_codes[g][:, i * P : (i + 1) * P].bitcast(E4M3),
                    lhsT_scale=down_scales[g][i][:],
                    rhs=codes[:].bitcast(E4M3),
                    rhs_scale=scales[:],
                    start=(g == h_first_pass[t] and i == 0),
                    stop=(g != h_first_pass[t] and i == PACK - 1),
                )

        def empty_h(t, engine):
            h_grouped[t] = sbuf(f"h{t}_grouped", [P, P, PACK], BF16)
            copy(engine, h_grouped[t][:], h_sums[t][:].rearrange("p i t -> p t i"))
            give_back(("h", t))

        def quantise_h(t):
            h_mx[t] = sbuf(f"h{t}_codes", [P, P], U32), sbuf(f"h{t}_scales", [P, P], U8)
            quantise(h_mx[t][0][:], h_mx[t][1][:], h_grouped[t][:])

        sums = {}
        results = sbuf("results", [P, T // P, N], F32)

        def base(t, n, passes=PASSES):
            for g in passes:
                opens = (t, n) not in sums
                if opens:
                    sums[t, n] = take_bank((t, n), f"sums{t}{n}", [P, HALF])
                codes, scales = x_mx[t, g]
                nc.tensor.matmul_mx(
                    out=sums[t, n][:],
                    lhsT=codes[:].bitcast(E4M3),
                    lhsT_scale=scales[:],
                    rhs=w4_codes[g][:, 2 * HALF * n : 2 * HALF * (n + 1)].bitcast(E2M1),
                    rhs_scale=w4_scale_rows[:, g, HALF * n : HALF * (n + 1)],
                    start=opens,
                    stop=False,
                )

        def branch(t, n, inside=0, width=HALF):
            codes, scales = h_mx[t]
            columns = slice(n * HALF + inside, n * HALF + inside + width)
            nc.tensor.matmul_mx(
                out=sums[t, n][:, inside : inside + width],
                lhsT=codes[:].bitcast(E4M3),
                lhsT_scale=scales[:],
                rhs=up_codes[:, columns].bitcast(E4M3),
                rhs_scale=up_scales[:, columns],
                start=False,
                stop=(inside + width == HALF),
            )

        def empty(t, n, engine):
            copy(engine, results[:, t, n * HALF : (n + 1) * HALF], sums[t, n][:])
            give_back((t, n))

        def piece(t, first, width, engine):
            bank = take_bank((t, "piece", first), f"piece{t}{first}", [P, width])
            for strip in range(0, width, P):
                column = first + strip
                for g in PASSES:
                    codes, scales = x_mx[t, g]
                    nc.tensor.matmul_mx(
                        out=bank[:, strip : strip + P],
                        lhsT=codes[:].bitcast(E4M3),
                        lhsT_scale=scales[:],
                        rhs=w4_codes[g][:, 2 * column : 2 * (column + P)].bitcast(E2M1),
                        rhs_scale=w4_scale_rows[:, g, column : column + P],
                        start=(strip == 0 and g == PASSES[0]),
                        stop=False,
                    )
            codes, scales = h_mx[t]
            nc.tensor.matmul_mx(
                out=bank[:],
                lhsT=codes[:].bitcast(E4M3),
                lhsT_scale=scales[:],
                rhs=up_codes[:, first : first + width].bitcast(E4M3),
                rhs_scale=up_scales[:, first : first + width],
                start=False,
                stop=True,
            )
            copy(engine, results[:, t, first : first + width], bank[:])
            give_back((t, "piece", first))

        def store(tiles, first, width):
            rows = out[tiles[0] * P : (tiles[-1] + 1) * P, first : first + width]
            nc.sync.dma_start(
                out=rows.rearrange("(t p) n -> p t n", p=P),
                in_=results[:, tiles[0] : tiles[-1] + 1, first : first + width],
            )

        nc.vector.memset(w4_scale_rows[:].rearrange("p g n -> p (g n)").bitcast(I32), 0)

        a, b = SECOND
        c, d = THIRD
        load_x(FIRST, 0)
        load_w4_scales()
        load_w4(0)
        load_down(0)
        load_down(1)
        load_x(FIRST[:2], 1)
        load_x(FIRST[2:], 1)
        load_w4(1)
        load_up(0)
        for g in PASSES:
            load_x(SECOND, g)
        load_up(1)
        for g in PASSES:
            load_x(THIRD, g)

        prepare_x(FIRST, 0, scalar_strips=1)
        for t in FIRST[:2]:
            base(t, 0, [0])
        copy_down(0)
        quantise_down(0)
        for t in FIRST:
            make_h(t, 0)
        for t in FIRST[2:]:
            base(t, 0, [0])
        copy_down(1)
        quantise_down(1, [0, 1])
        copy_x((1,), 1, SCALAR)
        copy_x((0,), 1, VECTOR)
        quantise_down(1, [2, 3])
        quantise_x((0,), 1)
        quantise_x((1,), 1)
        copy_x((3,), 1, SCALAR)
        copy_x((2,), 1, VECTOR)
        quantise_x((2,), 1)
        quantise_x((3,), 1)
        for t in FIRST[:2]:
            make_h(t, 1)
        for t in FIRST[:2]:
            base(t, 0, [1])
        for t in FIRST[2:]:
            make_h(t, 1)
            base(t, 0, [1])
        empty_h(0, SCALAR)
        empty_h(1, VECTOR)
        empty_h(2, SCALAR)
        for t in FIRST[:3]:
            base(t, 1)
        for t in FIRST[:2]:
            quantise_h(t)

        copy_up(VECTOR, 0, 256)
        copy_up(SCALAR, 384, 512)
        copy_up(VECTOR, 256, 384)
        empty_h(3, SCALAR)
        quantise_up(0, 256)
        quantise_up(256, 512)
        quantise_h(2)
        quantise_h(3)
        for inside in (0, QUARTER):
            for t in FIRST[:2]:
                branch(t, 0, inside, QUARTER)
        for g in PASSES:
            base(3, 1, [g])
            branch(2 + g, 0)
        copy_x((a,), 0, SCALAR)
        copy_x((b,), 0, VECTOR)
        copy_x((a,), 1, VECTOR)
        quantise_x((a,), 0)
        copy_x((b,), 1, VECTOR)
        quantise_x((a,), 1)
        quantise_x((b,), 0)
        quantise_x((b,), 1)
        empty(0, 0, SCALAR)
        empty(1, 0, SCALAR)
        empty(2, 0, VECTOR)
        empty(3, 0, SCALAR)
        for t in SECOND:
            for g in PASSES:
                make_h(t, g)
            base(t, 0)
        copy_up(SCALAR, 896, 1024)
        copy_up(VECTOR, 512, 768)
        copy_up(VECTOR, 768, 896)
        for t in SECOND:
            empty_h(t, SCALAR)
        quantise_up(512, 768)
        quantise_up(768, 1024)
        quantise_h(a)
        base(a, 1)
        for t in FIRST:
            branch(t, 1)
        for n in HALVES:
            branch(a, n)
        for t in THIRD:
            copy_x((t,), 0, VECTOR)
        quantise_h(b)
        for t in THIRD:
            copy_x((t,), 1, VECTOR)
        for t in THIRD:
            for g in PASSES:
                quantise_x((t,), g)
        for t in FIRST:
            empty(t, 1, SCALAR)
        for n in HALVES:
            empty(a, n, VECTOR)
        base(b, 1)
        for g in PASSES:
            make_h(c, g)
        for n in HALVES:
            branch(b, n)
        for g in PASSES:
            make_h(d, g)
        empty_h(c, VECTOR)
        for n in HALVES:
            empty(b, n, SCALAR)
        quantise_h(c)
        empty_h(d, VECTOR)
        quantise_h(d)
        base(c, 0)
        base(c, 1, [0])
        branch(c, 0)
        empty(c, 0, SCALAR)
        base(c, 1, [1])
        branch(c, 1)
        empty(c, 1, VECTOR)

        store(FIRST, 0, HALF)
        for t in FIRST:
            store((t,), HALF, HALF)
        for t in SECOND:
            store((t,), 0, N)
        for n in HALVES:
            store((c,), n * HALF, HALF)
        base(d, 0)
        branch(d, 0)
        empty(d, 0, SCALAR)
        store((d,), 0, HALF)
        piece(d, 512, QUARTER, VECTOR)
        store((d,), 512, QUARTER)
        piece(d, 768, P, SCALAR)
        piece(d, 896, P, VECTOR)
        store((d,), 768, QUARTER)
